import numpy as np, ml_dtypes
CORES = [5,29,101,125,133,157,229,253]
N = 8
import mx_ref
BF = ml_dtypes.bfloat16
def entries(a):
    return np.ascontiguousarray(a.T).reshape(-1)
def table(e):
    return np.ascontiguousarray(np.reshape(e, (-1, 16)).T).astype(np.int32)
def cols(t, e):
    v = np.concatenate([t.reshape(128, -1, 4), np.zeros((128, 1, 4), BF)], axis=1)
    return np.ascontiguousarray(v[:, e]).reshape(128, -1)
def cut(t, i, w=512):
    return t[:, w * i:w * i + w]
def f(rng, *shape):
    return mx_ref.flush((rng.standard_normal(shape, dtype=np.float32) * np.exp2(rng.integers(-2, 3, shape[:-1] + (1,)))).astype(BF))
def wide(rng, *shape, cols=0):
    v = rng.standard_normal(shape, dtype=np.float32) * np.exp2(rng.integers(-12, 13, shape)).astype(np.float32)
    if cols: v *= np.repeat(np.exp2(rng.integers(-cols, cols + 1, shape[:-2] + (1, shape[-1] // 4))) * (rng.random(shape[:-2] + (1, shape[-1] // 4)) > 0.0625), 4, axis=-1).astype(np.float32)
    return mx_ref.flush(v.astype(BF))
TB, T, CAPP, O = 256, 256, 32, 1
def lists(rng, case=""):
    o = []; odd = rng.permutation(N)
    for r in range(N):
        lo, hi = {"one": (1, 1), "full": (CAPP, CAPP), "runs": (1, CAPP // 2), "none": (1, CAPP)}.get(case, (0, CAPP))
        n = rng.integers(lo, hi + 1, N)
        if case == "none":
            if r == odd[0]: n[:] = 0; n[rng.integers(0, N)] = 1
            elif r == odd[1]: n[r] = 0
            elif r == odd[2]: n[np.arange(N) != r] = 0
            else: n[rng.permutation(N)[:rng.integers(1, N)]] = 0
        if n.sum() == 0: n[rng.integers(0, N)] = 1
        if case == "full": named = [np.append([0, TB - 1], 1 + rng.permutation(TB - 2)[:n[q] - 2]) for q in range(N)]
        else: named = [rng.permutation(TB)[:n[q]] for q in range(N)]
        pool = rng.permutation(np.concatenate([q * TB + named[q] for q in range(N)]))
        i = np.arange(len(pool))
        k = T - len(pool)
        i = np.concatenate([i, (rng.random(k) * rng.random(k) * len(pool)).astype(int)])
        i = np.sort(i) if case == "runs" else rng.permutation(i)
        o.append(table(pool[i]))
    return {"want": np.stack(o)}
def setup_inputs(rng):
    return {"x": f(rng, N, 128, 4 * TB), "w": f(rng, N, 128, 512 * O), **lists(rng)}
def setup_inputs_one(rng):
    return {**setup_inputs(rng), **lists(rng, "one")}
def setup_inputs_full(rng):
    return {**setup_inputs(rng), **lists(rng, "full")}
def setup_inputs_runs(rng):
    return {**setup_inputs(rng), **lists(rng, "runs")}
def setup_inputs_none(rng):
    return {**setup_inputs(rng), **lists(rng, "none")}
def setup_inputs_spread(rng):
    d = setup_inputs(rng); d["x"] = wide(rng, N, 128, 4 * TB, cols=8); return d
def check_inputs(d):
    b = []
    for r in range(N):
        e = entries(d["want"][r])
        if e.min() < 0 or e.max() >= N * TB or any(len(np.unique(e[e // TB == q])) > CAPP for q in range(N)): b.append("want")
    return b
def reference(x, w, want):
    every = np.concatenate([x[q] for q in range(N)], axis=1)
    y = np.zeros((N, 128, O * T), np.float32)
    for r in range(N):
        t = mx_ref.quantize(cols(every, entries(want[r])))
        for o in range(O):
            y[r][:, T * o:T * o + T] = mx_ref.matmul(mx_ref.quantize(np.ascontiguousarray(cut(w[r], o))), t)
    return {"y": y}

@@ -1,0 +1,369 @@
+from concourse.bass import DstId, RemoteDMATransfer
+from concourse.mybir import dt, AluOpType, ActivationFunctionType
+
+OP = AluOpType
+COPY = ActivationFunctionType.Copy
+XW = 272
+PW = 2432
+SMALL = {"allow_small_or_imprecise_dtypes": True}
+
+SCRATCH = {"wt": ("sbuf", [64, 16], "int32"), "hw": ("dram", [128, 2], "int32"),
+           "m0": ("psum", [128, 512], "float32"), "m1": ("psum", [128, 512], "float32")}
+for _t, _b in (("int32", "pi 1 pm 1 odd 1 w0 2"),
+               ("uint16", "w16 16 w2 32 jj 4 msg 4 la 6 lb 8 oa 8 ob 8 rl 2 rp 4 ou 16 oy 16"),
+               ("float32", "gsc 1 ua 16 fu 16 u1 16 u2 16 u3 16 nb 16 dd 16 ys 256 yo 256"),
+               ("bfloat16", "k0 2 z2 2 s0 1 s1 1 vwin 2048 pos %d cwin 2048 ones 256 cst 128 row 256 crow 272 rt 128 "
+                            "ne 832 sc 832 fr 128 qf 256 ge 256 gh 256 cc 256 le 512 nn 512 lg 64 lt 64 xt %d xs %d "
+                            "wb 512 ta 512 tb 512 vp 256 pr 512 pt 512" % (PW, 4 * XW, 4 * XW)),
+               ("float8_e4m3fn_x4", "qw 128 qa 128 qb 128 ca 128 cb 128 rc 32 ra 32"),
+               ("uint8", "pw 128 pa 128 pb 128 da 128 db 128 rs 32 rz 32")):
+    _w = _b.split()
+    for _i in range(0, len(_w), 2):
+        SCRATCH[_w[_i]] = ("sbuf", [128, int(_w[_i + 1])], _t)
+SEMAPHORES = "ld ldx ldw ld0 v s ps te aa ab ac ad own st su loc rl rp rc rs ra rz th tz tc hs oy".split()
+
+
+def plane_of(topo, cores, r):
+    return [k for k in range(len(cores)) if k == r or topo.same_plane(cores[k], cores[r])]
+
+
+def roads(topo, cores, r):
+    mine = plane_of(topo, cores, r)
+    far = [k for k in range(len(cores)) if k not in mine]
+    near = [None] + [k for k in mine if k != r]
+    c = cores[r]
+    able = [k for k in topo.cores_of(c) if k != c and all(topo.may_write(k, cores[f]) for f in far)]
+    able = [k for k in able if topo.die(k) == topo.die(c)] + [k for k in able if topo.die(k) != topo.die(c)]
+    a = mine.index(r)
+    return [(able[h], far[(h - a) % len(far)], near[h]) for h in range(len(far))]
+
+
+def mask(engines):
+    return sum(1 << k for k in engines)
+
+
+def xfer(topo, src_core, dst_core, engines, sem, src, dst):
+    rid, pid = topo.addr(dst_core, src_core)
+    return RemoteDMATransfer(dst_ids=[DstId(rid=rid, pnc=pid)], dma_engine_mask=mask(engines),
+                             remote_sem=sem, srcs=[src], dsts=[dst], alu_op=0)
+
+
+def u8(view):
+    return view.bitcast(dt.uint8)
+
+
+def relay(g, core, T, topo, r, h, f, near):
+    cores = T.cores
+    en = topo.engines(core, cores[f])
+    plane = plane_of(topo, cores, r)
+    far = [k for k in range(len(cores)) if k not in plane]
+    V, D, S = g.vector, g.sync, T.sem
+    n = [0]
+    left = [0]
+
+    def v(call):
+        call.then_inc(S.v, 1)
+        n[0] += 1
+
+    def vw():
+        V.wait_ge(S.v, n[0])
+
+    def send(k, sem, src, dst):
+        rid, pid = topo.addr(cores[k], core)
+        g.remote_dma(dst, src, sem, S.loc, pid, rid, mask(en))
+        left[0] += len(en)
+    if h < 2:
+        g.iota(T.pi[:, 0:1], [[0, 1]], 0, 1).then_inc(S.ps, 1)
+        V.wait_ge(S.ps, 1)
+        v(V.tensor_scalar(T.pm[:, :], T.pi[:, :], 15, None, OP.bitwise_and))
+        vw()
+        v(V.tensor_scalar(T.k0[:, 0:1], T.pm[:, :], 16.0 * h, None, OP.add))
+    else:
+        v(V.memset(T.k0[:, :], (0.0, 256.0)[h - 2]))
+    g.wait_ge(S.v, n[0])
+    where = (T.s0[:, 0:1], T.s1[:, 0:1], T.z2[:, 0:2], T.crow[:, 256:257])[h]
+    send(r, (S.th, S.th, S.tz, S.tc)[h], T.k0[:, 0:2 if h == 2 else 1], where)
+    if h == 0:
+        D.wait_ge(S.hs, 16)
+        for i in range(4):
+            D.dma_start(T.wt[16 * i:16 * i + 16, :], T.hw[:, :]).then_inc(S.ld, 16)
+        g.iota(T.nb[:, :], [[256, 8], [0, 2]], 0, 0, **SMALL).then_inc(S.ps, 1)
+        g.iota(T.dd[:, :], [[-224, 8], [16, 2]], 1792, 1, **SMALL).then_inc(S.ps, 1)
+        col = [32 * (plane.index(k) if k in plane else 4 + far.index(k)) for k in range(8)]
+        step = col[1] - col[0]
+        assert col == [col[0] + 32 * (k // 2) + step * (k % 2) for k in range(8)]
+        g.iota(T.vp[:, :], [[32, 4], [step, 2], [1, 32]], col[0], 0, **SMALL).then_inc(S.ps, 1)
+        v(V.memset(T.pos[:, 0:2048], 0.0))
+        V.wait_ge(S.ld, 64)
+        v(V.tensor_copy(T.w16[0:64, :], T.wt[:, :]))
+        v(V.tensor_copy(T.w16[64:128, :], T.wt[:, :]))
+        vw()
+        v(V.tensor_copy(T.w2[:, 0:32:2], T.w16[:, :]))
+        v(V.tensor_copy(T.w2[:, 1:32:2], T.w16[:, :]))
+        V.wait_ge(S.ps, 4)
+        V.wait_ge(S.rp, 4)
+        for b in range(4):
+            for a in range(4):
+                v(V.tensor_copy(T.ua[32 * a:32 * a + 32, 4 * b:4 * b + 4], T.rp[32 * b:32 * b + 32, :]))
+        vw()
+        v(V.tensor_scalar(T.fu[:, :], T.ua[:, :], 256.0, None, OP.is_ge))
+        v(V.tensor_tensor(T.u2[:, :], T.ua[:, :], T.nb[:, :], OP.add))
+        vw()
+        v(V.tensor_tensor(T.u1[:, :], T.fu[:, :], T.dd[:, :], OP.mult))
+        vw()
+        v(V.tensor_tensor(T.u3[:, :], T.u1[:, :], T.u2[:, :], OP.add))
+        vw()
+        v(V.tensor_copy(T.ou[:, :], T.u3[:, :]))
+        vw()
+        v(V.tensor_copy(T.pos[:, 0:PW].indirect(T.ou[:, 0:16]), T.vp[:, :]))
+        vw()
+        v(V.tensor_copy(T.pr[:, :], T.pos[:, 0:2048].indirect(T.w2[:, 0:32])))
+        vw()
+        v(V.transpose(T.pt[:, :], T.pr[:, :]))
+        vw()
+        v(V.tensor_copy(T.oy[:, :], T.pt[:, 0:512:32]))
+
+    def place(f):
+        return 2 * [k for _, k, _ in roads(topo, cores, f)].index(r)
+    g.wait_ge(S.rl, 4)
+    send(f, S.ab, T.rl[:, 0:2], T.lb[:, place(f):place(f) + 2])
+    if h == 0:
+        g.wait_ge(S.v, n[0])
+        send(r, S.oy, T.oy[:, 0:16], T.oy[:, 0:16])
+    here = slice(32 * plane.index(r), 32 * plane.index(r) + 32)
+    if near is not None:
+        g.wait_ge(S.ra, 4)
+        send(near, S.ac, u8(T.ra[:, :]), u8(T.ca[:, here]))
+        g.wait_ge(S.rz, 4)
+        send(near, S.ac, T.rz[:, :], T.da[:, here])
+    g.wait_ge(S.rc, 4)
+    send(f, S.ad, u8(T.rc[:, :]), u8(T.cb[:, here]))
+    g.wait_ge(S.rs, 4)
+    send(f, S.ad, T.rs[:, :], T.db[:, here])
+    g.wait_ge(S.loc, left[0])
+
+
+def rank_program(g, core, T, topo):
+    cores = T.cores
+    r = T.rank_of(core)
+    if r is None:
+        for k in range(len(cores)):
+            if core in topo.cores_of(cores[k]):
+                for h, (c, f, near) in enumerate(roads(topo, cores, k)):
+                    if c == core:
+                        relay(g, core, T, topo, k, h, f, near)
+        return
+    S = T.sem
+    plane = plane_of(topo, cores, r)
+    others = [k for k in plane if k != r]
+    road = roads(topo, cores, r)
+    me = plane.index(r)
+    h_rid, h_pid = topo.addr(road[0][0], core)
+    off = topo.engines(core, cores[others[0]])
+    on = topo.engines(core, road[0][0])
+    on = [e for e in on if e not in off] + off
+    V, A, D, P = g.vector, g.scalar, g.sync, g.tensor
+    n = {"v": 0, "s": 0, "ps": 0}
+
+    def count(name, call):
+        call.then_inc(S[name], 1)
+        n[name] += 1
+        return n[name]
+
+    def v(call):
+        return count("v", call)
+
+    def s(call):
+        return count("s", call)
+
+    def ps(call):
+        return count("ps", call)
+
+    def vw():
+        V.wait_ge(S.v, n["v"])
+
+    D.dma_start(T.wt[0:16, :], T.want[:, :]).then_inc(S.ld, 16)
+    A.dma_start(T.wt[16:32, :], T.want[:, :]).then_inc(S.ld, 16)
+    D.dma_start(T.wt[32:48, :], T.want[:, :]).then_inc(S.ld, 16)
+    A.dma_start(T.wt[48:64, :], T.want[:, :]).then_inc(S.ld, 16)
+    A.dma_start(T.w0[:, :], T.want[:, :]).then_inc(S.ld0, 16)
+    D.dma_start(T.xt[:, 0:1024], T.x[:, :]).then_inc(S.ldx, 16)
+    D.dma_start(T.wb[:, :], T.w[:, :]).then_inc(S.ldw, 16)
+
+    g_v = ps(g.iota(T.vwin[:, 0:128], [[1, 128]], 128, 0, **SMALL))
+    g_k = ps(g.iota(T.cst[0:32, 0:128], [[-32, 4], [0, 32]], 256, -1, **SMALL))
+    g_p = ps(g.iota(T.pi[:, 0:1], [[0, 1]], 0, 1))
+    g_c = ps(g.iota(T.cwin[:, 0:256], [[1, 256]], 0, 0, **SMALL))
+    g.wait_ge(S.ld0, 16)
+    g.remote_dma(T.hw[:, :], T.w0[:, 0:2], S.hs, S.loc, h_pid, h_rid, mask(on))
+
+    v(V.memset(T.ones[:, :], 1.0))
+    v(V.memset(T.xt[:, 1024:4 * XW], 0.0))
+    V.wait_ge(S.ps, g_v)
+    for k, f in ((128, 2.0), (256, 4.0)):
+        v_v = v(V.tensor_scalar(T.vwin[:, k:2 * k], T.vwin[:, 0:k], f, None, OP.mult))
+        vw()
+    v(V.tensor_scalar(T.vwin[:, 512:1024], T.vwin[:, 0:512], 16.0, None, OP.mult))
+    v(V.tensor_scalar(T.vwin[:, 1024:1536], T.vwin[:, 0:512], 256.0, None, OP.mult))
+    A.wait_ge(S.v, v_v)
+    s_v = s(A.activation(T.vwin[:, 1536:2048], T.vwin[:, 0:512], COPY, scale=4096.0))
+    V.wait_ge(S.ps, g_k)
+    v_k = v(V.tensor_copy(T.cst[32:64, :], T.cst[0:32, :]))
+    V.wait_ge(S.ps, g_p)
+    v(V.tensor_scalar(T.odd[:, :], T.pi[:, :], 4, 1, OP.arith_shift_right, OP.bitwise_and))
+    V.wait_ge(S.v, v_k)
+    v(V.tensor_scalar(T.cst[64:128, :], T.cst[0:64, :], -128.0, None, OP.add))
+
+    V.wait_ge(S.ld, 64)
+    v(V.tensor_copy(T.w16[0:64, :], T.wt[:, :]))
+    v_w = v(V.tensor_copy(T.w16[64:128, :], T.wt[:, :]))
+    V.wait_ge(S.s, s_v)
+    vw()
+    v_r = v(V.tensor_copy(T.row[:, 128:256], T.vwin[:, 0:2048].indirect(T.w16[:, 8:16])))
+    A.wait_ge(S.v, v_w)
+    A.wait_ge(S.s, s_v)
+    s_r = s(A.activation(T.row[:, 0:128], T.vwin[:, 0:2048].indirect(T.w16[:, 0:8]), COPY))
+    for a in range(4):
+        q = slice(32 * a, 32 * a + 32)
+        v(V.tensor_scalar(T.gsc[q, :], T.odd[q, :], -0.75 * 16.0 ** -a, 16.0 ** -a, OP.mult, OP.add))
+
+    A.wait_ge(S.ps, g_c)
+    for k in (256, 512, 1024):
+        k_s = s(A.activation(T.cwin[:, k:2 * k], T.cwin[:, 0:k], COPY))
+        A.wait_ge(S.s, k_s)
+    s_cr = s(A.activation(T.crow[:, 0:256], T.cwin[:, 0:2048].indirect(T.w16[:, 0:16]), COPY))
+    A.wait_ge(S.ldx, 16)
+    for t in range(4):
+        s_xs = s(A.activation(T.xs[:, XW * t:XW * t + XW], T.xt[:, t:4 * XW:4], COPY))
+
+    V.wait_ge(S.v, v_r)
+    V.wait_ge(S.s, s_r)
+    halves = [slice(64 * h, 64 * h + 64) for h in range(2)]
+    for h in range(2):
+        v(V.transpose(T.rt[halves[h], 0:128], T.row[halves[h], 128 * h:128 * h + 128]))
+    vw()
+    at = [0]
+    for b in range(4):
+        at.append(at[b] + 256 - 32 * b)
+    ne = [v(V.tensor_scalar(T.ne[:, at[b]:at[b + 1]], T.row[:, 32 * b:256], T.rt[:, 32 * b:32 * b + 1], None, OP.not_equal))
+          for b in range(4)]
+    sc = []
+    for b in range(4):
+        V.wait_ge(S.v, ne[b])
+        sc.append(v(V.tensor_tensor_scan(T.sc[:, at[b]:at[b + 1]], T.ne[:, at[b]:at[b + 1]], T.ones[:, 0:256 - 32 * b],
+                                         0.0, OP.mult, OP.add)))
+    for b in range(4):
+        V.wait_ge(S.v, sc[b])
+        v(V.tensor_scalar(T.fr[:, 32 * b:32 * b + 32], T.cst[:, 32 * b:32 * b + 32], T.sc[:, at[b + 1] - 1:at[b + 1]],
+                          T.rt[:, 32 * b:32 * b + 1], OP.is_equal, OP.mult))
+    vw()
+    qf = [v(V.transpose(T.qf[halves[h], 128 * h:128 * h + 128], T.fr[halves[h], 0:128])) for h in range(2)]
+    for h in range(2):
+        V.wait_ge(S.v, qf[h])
+        v(V.tensor_copy(T.qf[halves[1 - h], 128 * h:128 * h + 128], T.qf[halves[h], 128 * h:128 * h + 128]))
+    vw()
+    v(V.tensor_scalar(T.ge[:, :], T.qf[:, :], T.gsc[:, 0:1], 128.0, OP.mult, OP.is_ge))
+    v(V.tensor_scalar(T.gh[:, :], T.qf[:, :], T.gsc[:, 0:1], 512.0, OP.mult, OP.is_ge))
+    vw()
+    v(V.tensor_tensor_scan(T.cc[:, :], T.ge[:, :], T.gh[:, :], 0.0, OP.add, OP.subtract))
+    V.wait_ge(S.th, 16)
+    vw()
+    le, nn = [], []
+    for k, t in enumerate((T.s0, T.s1)):
+        le.append(v(V.tensor_scalar(T.le[:, 256 * k:256 * k + 256], T.cc[:, :], t[:, 0:1], None, OP.is_le)))
+    for k in range(2):
+        V.wait_ge(S.v, le[k])
+        nn.append(v(V.tensor_tensor_scan(T.nn[:, 256 * k:256 * k + 256], T.ones[:, :], T.le[:, 256 * k:256 * k + 256],
+                                         0.0, OP.mult, OP.add)))
+    V.wait_ge(S.tz, 8)
+    for k in range(2):
+        V.wait_ge(S.v, nn[k])
+        v(V.tensor_scalar(T.jj[:, 2 * k:2 * k + 2], T.z2[:, :], T.nn[:, 256 * k + 255:256 * k + 256], None, OP.add))
+    V.wait_ge(S.tc, 8)
+    V.wait_ge(S.s, s_cr)
+    vw()
+    v(V.tensor_copy(T.lg[:, :], T.crow[:, 0:257].indirect(T.jj[:, 0:4])))
+    vw()
+    v(V.transpose(T.lt[:, :], T.lg[:, :]))
+    vw()
+    for k in range(2):
+        v_msg = v(V.tensor_copy(T.msg[:, 2 * k:2 * k + 2], T.lt[:, 16 * k:64:32]))
+
+    def of(f):
+        return T.msg[:, 2 * (f % 2):2 * (f % 2) + 2]
+
+    def among(f):
+        return 2 * [k for k in plane if k != f].index(r)
+    g.wait_ge(S.v, v_msg)
+    g.remote_dma_fused([xfer(topo, core, c, on[4 * i:4 * i + 4], S.rl, of(f), T.rl[:, 0:2])
+                        for i, (c, f, _) in enumerate(road)], local_sem=S.loc)
+    g.remote_dma_fused([xfer(topo, core, cores[f], off[2 * i:2 * i + 2], S.aa, of(f), T.la[:, among(f):among(f) + 2])
+                        for i, f in enumerate(others)], local_sem=S.loc)
+    g.remote_dma(T.rp[:, 0:4], T.msg[:, 0:4], S.rp, S.loc, h_pid, h_rid, mask(on[0:4]))
+
+    V.wait_ge(S.ldw, 16)
+    v_qw = v(V.quantize_mx(T.qw[:, :], T.pw[:, :], T.wb[:, :]))
+    mq = slice(32 * (r // 2), 32 * (r // 2) + 32)
+    V.wait_ge(S.v, v_msg)
+    for a in range(4):
+        v(V.tensor_copy(T.oa[32 * a:32 * a + 32, 0:2], T.msg[mq, 2 * (r % 2):2 * (r % 2) + 2]))
+
+    def serve(lists, offs, o0, tile, codes, plane8, sem, arrivals):
+        V.wait_ge(sem, arrivals)
+        for a in range(4):
+            v_o = v(V.tensor_copy(offs[32 * a:32 * a + 32, o0:8], lists[mq, :]))
+        vw()
+        for t in range(2):
+            v(V.tensor_copy(tile[:, t:512:4], T.xs[:, XW * t:XW * t + XW].indirect(offs[:, 0:8])))
+        A.wait_ge(S.v, v_o)
+        for t in range(2, 4):
+            s_t = s(A.activation(tile[:, t:512:4], T.xs[:, XW * t:XW * t + XW].indirect(offs[:, 0:8]), COPY))
+        vw()
+        V.wait_ge(S.s, s_t)
+        return v(V.quantize_mx(codes[:, :], plane8[:, :], tile[:, :]))
+
+    V.wait_ge(S.s, s_xs)
+    A.wait_ge(S.s, s_xs)
+    v_qa = serve(T.la, T.oa, 2, T.ta, T.qa, T.pa, S.aa, 6)
+    v_qb = serve(T.lb, T.ob, 0, T.tb, T.qb, T.pb, S.ab, 32)
+
+    def codes(q, i):
+        return u8(q[:, 32 * i:32 * i + 32])
+
+    def scales(p, i):
+        return p[:, 32 * i:32 * i + 32]
+    for done, first, view, src, dst, sem in ((v_qa, 1, codes, T.qa, T.ra, S.ra), (v_qa, 1, scales, T.pa, T.rz, S.rz),
+                                             (v_qb, 0, codes, T.qb, T.rc, S.rc), (v_qb, 0, scales, T.pb, T.rs, S.rs)):
+        g.wait_ge(S.v, done)
+        g.remote_dma_fused([xfer(topo, core, road[h][0], on[4 * h:4 * h + 4], sem, view(src, h), view(dst, 0))
+                            for h in range(first, 4)], local_sem=S.loc)
+    g.wait_ge(S.loc, 16 + 16 + 6 + 4 + 2 * 12 + 2 * 16)
+    here = slice(32 * me, 32 * me + 32)
+    D.wait_ge(S.v, v_qa)
+    D.dma_start(u8(T.ca[:, here]), u8(T.qa[:, 0:32])).then_inc(S.own, 16)
+    D.dma_start(T.da[:, here], T.pa[:, 0:32]).then_inc(S.own, 16)
+
+    P.wait_ge(S.v, v_qw)
+    P.wait_ge(S.ac, 48)
+    P.wait_ge(S.own, 32)
+    P.matmul_mx(T.m0[:, 0:128], T.qw[:, :], T.pw[:, :], T.ca[:, :], T.da[:, :], True, True).then_inc(S.te, 1)
+    P.wait_ge(S.ad, 64)
+    P.matmul_mx(T.m1[:, 0:128], T.qw[:, :], T.pw[:, :], T.cb[:, :], T.db[:, :], True, True).then_inc(S.te, 1)
+    A.wait_ge(S.te, 1)
+    s_y = s(A.activation(T.ys[:, 0:128], T.m0[:, 0:128], COPY))
+    V.wait_ge(S.oy, 8)
+    A.wait_ge(S.oy, 8)
+    V.wait_ge(S.te, 2)
+    v_y = v(V.tensor_copy(T.ys[:, 128:256], T.m1[:, 0:128]))
+    vw()
+    V.wait_ge(S.s, s_y)
+    v_o = v(V.tensor_copy(T.yo[:, 0:128], T.ys[:, 0:256].indirect(T.oy[:, 0:8])))
+    A.wait_ge(S.v, v_y)
+    A.wait_ge(S.s, s_y)
+    s_o = s(A.activation(T.yo[:, 128:256], T.ys[:, 0:256].indirect(T.oy[:, 8:16]), COPY))
+    D.wait_ge(S.v, v_o)
+    D.dma_start(T.y[:, 0:128], T.yo[:, 0:128]).then_inc(S.st, 16)
+    A.wait_ge(S.s, s_o)
+    A.dma_start(T.y[:, 128:256], T.yo[:, 128:256]).then_inc(S.su, 16)
+    D.wait_ge(S.st, 16)
+    A.wait_ge(S.su, 16)

@@ -2,25 +2,28 @@ from concourse.bass import DstId, RemoteDMATransfer
 from concourse.mybir import dt, AluOpType, ActivationFunctionType
 
 OP = AluOpType
-COPY = ActivationFunctionType.Copy
-XW = 272
-PW = 2432
+ACT = ActivationFunctionType
+COPY = ACT.Copy
+XW = 384
+PO = 32 + XW
 SMALL = {"allow_small_or_imprecise_dtypes": True}
 
 SCRATCH = {"wt": ("sbuf", [64, 16], "int32"), "hw": ("dram", [128, 2], "int32"),
            "m0": ("psum", [128, 512], "float32"), "m1": ("psum", [128, 512], "float32")}
-for _t, _b in (("int32", "pi 1 pm 1 odd 1 w0 2"),
-               ("uint16", "w16 16 w2 32 jj 4 msg 4 la 6 lb 8 oa 8 ob 8 rl 2 rp 4 ou 16 oy 16"),
-               ("float32", "gsc 1 ua 16 fu 16 u1 16 u2 16 u3 16 nb 16 dd 16 ys 256 yo 256"),
-               ("bfloat16", "k0 2 z2 2 s0 1 s1 1 vwin 2048 pos %d cwin 2048 ones 256 cst 128 row 256 crow 272 rt 128 "
-                            "ne 832 sc 832 fr 128 qf 256 ge 256 gh 256 cc 256 le 512 nn 512 lg 64 lt 64 xt %d xs %d "
-                            "wb 512 ta 512 tb 512 vp 256 pr 512 pt 512" % (PW, 4 * XW, 4 * XW)),
-               ("float8_e4m3fn_x4", "qw 128 qa 128 qb 128 ca 128 cb 128 rc 32 ra 32"),
-               ("uint8", "pw 128 pa 128 pb 128 da 128 db 128 rs 32 rz 32")):
+for _t, _b in (("int32", "pi 1 pm 1 w0 2 ec 16 eq 16"),
+               ("uint16", "w16 16 w2 32 jj 4 oo 16 ou 4 oy 16"),
+               ("float32", "acc 1 e1 16 e2 16 e3 16 e4 16 b1 4 b2 4 b3 4 ys 256 yo 256"),
+               ("bfloat16", "k0 2 hf 2 s0 1 s1 1 gsc 1 vwin 2336 pos %d row 256 rt 256 ne 640 sc 640 fr 128 qf 272 "
+                            "ge 256 gh 256 cc 256 le 256 nn 256 sg 256 lg 64 lt 64 li 14 rl 4 xt 1024 xs %d "
+                            "wb 512 ta 512 tb 512 vp 64 pr 512 pt 512 p2 16 p3 16" % (8 * PO, 4 * XW)),
+               ("float8_e4m3fn_x4", "qw 128 qa 128 ca 128 cb 224 rc 64"),
+               ("uint8", "pw 128 pa 128 da 128 db 224 rs 64")):
     _w = _b.split()
     for _i in range(0, len(_w), 2):
         SCRATCH[_w[_i]] = ("sbuf", [128, int(_w[_i + 1])], _t)
-SEMAPHORES = "ld ldx ldw ld0 v s ps te aa ab ac ad own st su loc rl rp rc rs ra rz th tz tc hs oy".split()
+SEMAPHORES = "ld ldx ldw ld0 v s ps te la ac ad st su loc rl rp rc rs th tz tc hs oy".split()
+QUARTERS = [slice(32 * a, 32 * a + 32) for a in range(4)]
+LOW, HIGH = slice(0, 64), slice(64, 128)
 
 
 def plane_of(topo, cores, r):
@@ -30,12 +33,18 @@ def plane_of(topo, cores, r):
 def roads(topo, cores, r):
     mine = plane_of(topo, cores, r)
     far = [k for k in range(len(cores)) if k not in mine]
-    near = [None] + [k for k in mine if k != r]
     c = cores[r]
     able = [k for k in topo.cores_of(c) if k != c and all(topo.may_write(k, cores[f]) for f in far)]
-    able = [k for k in able if topo.die(k) == topo.die(c)] + [k for k in able if topo.die(k) != topo.die(c)]
+    same = [k for k in able if topo.die(k) == topo.die(c)]
+    other = [k for k in able if topo.die(k) != topo.die(c)]
     a = mine.index(r)
-    return [(able[h], far[(h - a) % len(far)], near[h]) for h in range(len(far))]
+    f = [far[(h - a) % 4] for h in range(4)]
+    m = [mine[(a + j) % 4] for j in range(4)]
+    return [same[0], other[0], same[1], other[1]], [f[0], m[1], f[1], m[2], f[2], f[3], m[3], r]
+
+
+RUNS = ((0, 1), (2, 3), (4,), (5,))
+PLACES = 2
 
 
 def mask(engines):
@@ -52,12 +61,24 @@ def u8(view):
     return view.bitcast(dt.uint8)
 
 
-def relay(g, core, T, topo, r, h, f, near):
+def landing(T, run):
+    if run < 4:
+        at = slice(32 * run, 32 * run + 32)
+        return T.ca[:, at], T.da[:, at], T.sem.ac
+    at = slice(32 * run, 32 * run + 32)
+    return T.cb[:, at], T.db[:, at], T.sem.ad
+
+
+def column(run):
+    return 32 * run if run < 4 else 128 + 32 * ((run - 3) % 4 if run < 7 else 0)
+
+
+def relay(g, core, T, topo, r, h):
     cores = T.cores
+    slots = roads(topo, cores, r)[1]
+    f = slots[RUNS[h][0]]
     en = topo.engines(core, cores[f])
-    plane = plane_of(topo, cores, r)
-    far = [k for k in range(len(cores)) if k not in plane]
-    V, D, S = g.vector, g.sync, T.sem
+    V, A, D, S = g.vector, g.scalar, g.sync, T.sem
     n = [0]
     left = [0]
 
@@ -72,74 +93,92 @@ def relay(g, core, T, topo, r, h, f, near):
         rid, pid = topo.addr(cores[k], core)
         g.remote_dma(dst, src, sem, S.loc, pid, rid, mask(en))
         left[0] += len(en)
-    if h < 2:
+    if h == PLACES:
+        v(V.memset(T.k0[:, :], 0.5))
+    else:
         g.iota(T.pi[:, 0:1], [[0, 1]], 0, 1).then_inc(S.ps, 1)
         V.wait_ge(S.ps, 1)
-        v(V.tensor_scalar(T.pm[:, :], T.pi[:, :], 15, None, OP.bitwise_and))
-        vw()
-        v(V.tensor_scalar(T.k0[:, 0:1], T.pm[:, :], 16.0 * h, None, OP.add))
-    else:
-        v(V.memset(T.k0[:, :], (0.0, 256.0)[h - 2]))
+        if h < 2:
+            v(V.tensor_scalar(T.pm[:, :], T.pi[:, :], 15, None, OP.bitwise_and))
+            vw()
+            v(V.tensor_scalar(T.k0[:, 0:1], T.pm[:, :], 16.5 * h, None, OP.add))
+        else:
+            v(V.tensor_scalar(T.pm[:, :], T.pi[:, :], 4, 1, OP.arith_shift_right, OP.bitwise_and))
+            vw()
+            for a, q in enumerate(QUARTERS):
+                v(V.tensor_scalar(T.k0[q, 0:1], T.pm[q, :], -0.75 * 16.0 ** -a, 16.0 ** -a, OP.mult, OP.add))
     g.wait_ge(S.v, n[0])
-    where = (T.s0[:, 0:1], T.s1[:, 0:1], T.z2[:, 0:2], T.crow[:, 256:257])[h]
-    send(r, (S.th, S.th, S.tz, S.tc)[h], T.k0[:, 0:2 if h == 2 else 1], where)
-    if h == 0:
+    where = (T.s0[:, 0:1], T.s1[:, 0:1], T.hf[:, 0:2], T.gsc[:, 0:1])[h]
+    send(r, (S.th, S.th, S.tz, S.tc)[h], T.k0[:, 0:2 if h == PLACES else 1], where)
+    if h == PLACES:
         D.wait_ge(S.hs, 16)
         for i in range(4):
             D.dma_start(T.wt[16 * i:16 * i + 16, :], T.hw[:, :]).then_inc(S.ld, 16)
-        g.iota(T.nb[:, :], [[256, 8], [0, 2]], 0, 0, **SMALL).then_inc(S.ps, 1)
-        g.iota(T.dd[:, :], [[-224, 8], [16, 2]], 1792, 1, **SMALL).then_inc(S.ps, 1)
-        col = [32 * (plane.index(k) if k in plane else 4 + far.index(k)) for k in range(8)]
-        step = col[1] - col[0]
-        assert col == [col[0] + 32 * (k // 2) + step * (k % 2) for k in range(8)]
-        g.iota(T.vp[:, :], [[32, 4], [step, 2], [1, 32]], col[0], 0, **SMALL).then_inc(S.ps, 1)
-        v(V.memset(T.pos[:, 0:2048], 0.0))
+        g.iota(T.pi[:, 0:1], [[0, 1]], 0, 1).then_inc(S.ps, 1)
+        g.wait_ge(S.ps, 1)
+        col = [column(roads(topo, cores, q)[1].index(r)) for q in range(8)]
+        for a, q in enumerate(QUARTERS):
+            g.iota(T.b1[q, :], [[PO, 2], [0, 2]], 2 * a * PO + 32, 0, **SMALL).then_inc(S.ps, 1)
+            g.iota(T.b3[q, :], [[PO, 2], [16, 2]], 2 * a * PO, 0, **SMALL).then_inc(S.ps, 1)
+            g.iota(T.vp[q, :], [[col[2 * a + 1] - col[2 * a], 2], [1, 32]], col[2 * a], 0, **SMALL).then_inc(S.ps, 1)
+        v(V.memset(T.pos[:, :], 0.0))
+        V.wait_ge(S.ps, 13)
+        v(V.tensor_scalar(T.pm[:, :], T.pi[:, :], 15, None, OP.bitwise_and))
+        vw()
+        v(V.tensor_copy(T.acc[:, :], T.pm[:, :]))
+        vw()
+        v(V.tensor_scalar(T.b2[:, :], T.b3[:, :], T.acc[:, 0:1], None, OP.add))
         V.wait_ge(S.ld, 64)
-        v(V.tensor_copy(T.w16[0:64, :], T.wt[:, :]))
-        v(V.tensor_copy(T.w16[64:128, :], T.wt[:, :]))
+        v(V.tensor_scalar(T.ec[LOW, :], T.wt[:, :], 255, None, OP.bitwise_and))
+        v(V.tensor_scalar(T.eq[LOW, :], T.wt[:, :], 8, None, OP.arith_shift_right))
         vw()
-        v(V.tensor_copy(T.w2[:, 0:32:2], T.w16[:, :]))
-        v(V.tensor_copy(T.w2[:, 1:32:2], T.w16[:, :]))
-        V.wait_ge(S.ps, 4)
-        V.wait_ge(S.rp, 4)
-        for b in range(4):
-            for a in range(4):
-                v(V.tensor_copy(T.ua[32 * a:32 * a + 32, 4 * b:4 * b + 4], T.rp[32 * b:32 * b + 32, :]))
+        v(V.tensor_scalar(T.e1[LOW, :], T.ec[LOW, :], 2.0, -128.0, OP.mult, OP.add))
+        v(V.tensor_scalar(T.e2[LOW, :], T.eq[LOW, :], float(PO), 32.0, OP.mult, OP.add))
         vw()
-        v(V.tensor_scalar(T.fu[:, :], T.ua[:, :], 256.0, None, OP.is_ge))
-        v(V.tensor_tensor(T.u2[:, :], T.ua[:, :], T.nb[:, :], OP.add))
+        v(V.tensor_tensor(T.e3[LOW, :], T.e1[LOW, :], T.ec[LOW, :], OP.max))
         vw()
-        v(V.tensor_tensor(T.u1[:, :], T.fu[:, :], T.dd[:, :], OP.mult))
+        v(V.tensor_tensor(T.e4[LOW, :], T.e3[LOW, :], T.e2[LOW, :], OP.add))
         vw()
-        v(V.tensor_tensor(T.u3[:, :], T.u1[:, :], T.u2[:, :], OP.add))
+        for half in (LOW, HIGH):
+            for k in range(2):
+                v(V.tensor_copy(T.w2[half, k:32:2], T.e4[LOW, :]))
+        V.wait_ge(S.rl, 4)
+        V.wait_ge(S.rp, 8)
         vw()
-        v(V.tensor_copy(T.ou[:, :], T.u3[:, :]))
+        for k in range(4):
+            v(V.tensor_scalar(T.ou[:, k:k + 1], T.rl[:, k:k + 1], T.b1[:, k:k + 1], T.b2[:, k:k + 1], OP.add, OP.max))
         vw()
-        v(V.tensor_copy(T.pos[:, 0:PW].indirect(T.ou[:, 0:16]), T.vp[:, :]))
+        v(V.tensor_copy(T.pos[:, :].indirect(T.ou[:, 0:4]), T.vp[:, :]))
+        A.wait_ge(S.v, n[0])
+        A.activation(T.pr[:, 256:512], T.pos[:, :].indirect(T.w2[:, 16:32]), COPY).then_inc(S.s, 1)
         vw()
-        v(V.tensor_copy(T.pr[:, :], T.pos[:, 0:2048].indirect(T.w2[:, 0:32])))
+        v(V.tensor_copy(T.pr[:, 0:256], T.pos[:, :].indirect(T.w2[:, 0:16])))
         vw()
-        v(V.transpose(T.pt[:, :], T.pr[:, :]))
+        v(V.transpose(T.pt[:, 0:256], T.pr[:, 0:256]))
+        V.wait_ge(S.s, 1)
+        v(V.transpose(T.pt[:, 256:512], T.pr[:, 256:512]))
         vw()
-        v(V.tensor_copy(T.oy[:, :], T.pt[:, 0:512:32]))
+        v(V.tensor_tensor(T.p2[LOW, :], T.pt[LOW, 0:512:32], T.pt[HIGH, 0:512:32], OP.add))
+        vw()
+        v(V.tensor_tensor(T.p3[QUARTERS[0], :], T.p2[QUARTERS[0], :], T.p2[QUARTERS[1], :], OP.add))
+        vw()
+        for q in QUARTERS:
+            v(V.tensor_copy(T.oy[q, :], T.p3[QUARTERS[0], :]))
 
-    def place(f):
-        return 2 * [k for _, k, _ in roads(topo, cores, f)].index(r)
+    at = 2 * roads(topo, cores, f)[1].index(r)
     g.wait_ge(S.rl, 4)
-    send(f, S.ab, T.rl[:, 0:2], T.lb[:, place(f):place(f) + 2])
-    if h == 0:
+    send(f, S.la, T.rl[:, 2 * (f % 2):2 * (f % 2) + 2], T.li[:, at:at + 2])
+    if h == PLACES:
+        g.wait_ge(S.rp, 8)
         g.wait_ge(S.v, n[0])
         send(r, S.oy, T.oy[:, 0:16], T.oy[:, 0:16])
-    here = slice(32 * plane.index(r), 32 * plane.index(r) + 32)
-    if near is not None:
-        g.wait_ge(S.ra, 4)
-        send(near, S.ac, u8(T.ra[:, :]), u8(T.ca[:, here]))
-        g.wait_ge(S.rz, 4)
-        send(near, S.ac, T.rz[:, :], T.da[:, here])
-    g.wait_ge(S.rc, 4)
-    send(f, S.ad, u8(T.rc[:, :]), u8(T.cb[:, here]))
-    g.wait_ge(S.rs, 4)
-    send(f, S.ad, T.rs[:, :], T.db[:, here])
+    share = len(en) // len(RUNS[h])
+    for part, (sem, buf, view) in enumerate(((S.rc, T.rc, u8), (S.rs, T.rs, lambda a: a))):
+        g.wait_ge(sem, 8)
+        g.remote_dma_fused([xfer(topo, core, cores[slots[run]], en[share * i:share * i + share], landing(T, run)[2],
+                                 view(buf[:, 32 * i:32 * i + 32]), view(landing(T, run)[part]))
+                            for i, run in enumerate(RUNS[h])], local_sem=S.loc)
+        left[0] += len(en)
     g.wait_ge(S.loc, left[0])
 
 
@@ -149,21 +188,19 @@ def rank_program(g, core, T, topo):
     if r is None:
         for k in range(len(cores)):
             if core in topo.cores_of(cores[k]):
-                for h, (c, f, near) in enumerate(roads(topo, cores, k)):
+                for h, c in enumerate(roads(topo, cores, k)[0]):
                     if c == core:
-                        relay(g, core, T, topo, k, h, f, near)
+                        relay(g, core, T, topo, k, h)
         return
     S = T.sem
-    plane = plane_of(topo, cores, r)
-    others = [k for k in plane if k != r]
-    road = roads(topo, cores, r)
-    me = plane.index(r)
-    h_rid, h_pid = topo.addr(road[0][0], core)
-    off = topo.engines(core, cores[others[0]])
-    on = topo.engines(core, road[0][0])
+    relays, slots = roads(topo, cores, r)
+    assert all((k in plane_of(topo, cores, r)) == (k % 2 == r % 2) for k in range(8))
+    h_rid, h_pid = topo.addr(relays[PLACES], core)
+    off = topo.engines(core, cores[slots[6]])
+    on = topo.engines(core, relays[0])
     on = [e for e in on if e not in off] + off
     V, A, D, P = g.vector, g.scalar, g.sync, g.tensor
-    n = {"v": 0, "s": 0, "ps": 0}
+    n = {"v": 0, "s": 0, "ps": 0, "loc": 0}
 
     def count(name, call):
         call.then_inc(S[name], 1)
@@ -182,23 +219,30 @@ def rank_program(g, core, T, topo):
     def vw():
         V.wait_ge(S.v, n["v"])
 
+    def send(transfers):
+        g.remote_dma_fused([xfer(topo, core, *t) for t in transfers], local_sem=S.loc)
+        n["loc"] += sum(len(t[1]) for t in transfers)
+
     D.dma_start(T.wt[0:16, :], T.want[:, :]).then_inc(S.ld, 16)
     A.dma_start(T.wt[16:32, :], T.want[:, :]).then_inc(S.ld, 16)
     D.dma_start(T.wt[32:48, :], T.want[:, :]).then_inc(S.ld, 16)
     A.dma_start(T.wt[48:64, :], T.want[:, :]).then_inc(S.ld, 16)
-    A.dma_start(T.w0[:, :], T.want[:, :]).then_inc(S.ld0, 16)
-    D.dma_start(T.xt[:, 0:1024], T.x[:, :]).then_inc(S.ldx, 16)
+    D.dma_start(T.w0[:, :], T.want[:, :]).then_inc(S.ld0, 16)
+    D.dma_start(T.xt[:, :], T.x[:, :]).then_inc(S.ldx, 16)
     D.dma_start(T.wb[:, :], T.w[:, :]).then_inc(S.ldw, 16)
 
+    tri = 2048
     g_v = ps(g.iota(T.vwin[:, 0:128], [[1, 128]], 128, 0, **SMALL))
-    g_k = ps(g.iota(T.cst[0:32, 0:128], [[-32, 4], [0, 32]], 256, -1, **SMALL))
-    g_p = ps(g.iota(T.pi[:, 0:1], [[0, 1]], 0, 1))
-    g_c = ps(g.iota(T.cwin[:, 0:256], [[1, 256]], 0, 0, **SMALL))
+    v_z = v(V.memset(T.vwin[:, tri:tri + 288], 0.0))
+    g.wait_ge(S.v, v_z)
+    g.wait_ge(S.ps, g_v)
+    for q in QUARTERS[0:2]:
+        g_t = ps(g.affine_select(T.vwin[q, tri:tri + 32], T.vwin[q, tri:tri + 32], [[-1, 32]], OP.not_equal, 1.0, 0, 1))
     g.wait_ge(S.ld0, 16)
-    g.remote_dma(T.hw[:, :], T.w0[:, 0:2], S.hs, S.loc, h_pid, h_rid, mask(on))
+    send([(relays[PLACES], on, S.hs, T.w0[:, 0:2], T.hw[:, :])])
 
-    v(V.memset(T.ones[:, :], 1.0))
-    v(V.memset(T.xt[:, 1024:4 * XW], 0.0))
+    v(V.memset(T.qf[:, 256:272], 0.0))
+    v(V.memset(T.w16[HIGH, 14:16], tri))
     V.wait_ge(S.ps, g_v)
     for k, f in ((128, 2.0), (256, 4.0)):
         v_v = v(V.tensor_scalar(T.vwin[:, k:2 * k], T.vwin[:, 0:k], f, None, OP.mult))
@@ -207,148 +251,133 @@ def rank_program(g, core, T, topo):
     v(V.tensor_scalar(T.vwin[:, 1024:1536], T.vwin[:, 0:512], 256.0, None, OP.mult))
     A.wait_ge(S.v, v_v)
     s_v = s(A.activation(T.vwin[:, 1536:2048], T.vwin[:, 0:512], COPY, scale=4096.0))
-    V.wait_ge(S.ps, g_k)
-    v_k = v(V.tensor_copy(T.cst[32:64, :], T.cst[0:32, :]))
-    V.wait_ge(S.ps, g_p)
-    v(V.tensor_scalar(T.odd[:, :], T.pi[:, :], 4, 1, OP.arith_shift_right, OP.bitwise_and))
-    V.wait_ge(S.v, v_k)
-    v(V.tensor_scalar(T.cst[64:128, :], T.cst[0:64, :], -128.0, None, OP.add))
+    V.wait_ge(S.ps, g_t)
+    v(V.tensor_copy(T.vwin[HIGH, tri:tri + 32], T.vwin[LOW, tri:tri + 32]))
 
     V.wait_ge(S.ld, 64)
-    v(V.tensor_copy(T.w16[0:64, :], T.wt[:, :]))
-    v_w = v(V.tensor_copy(T.w16[64:128, :], T.wt[:, :]))
+    v(V.tensor_copy(T.w16[LOW, :], T.wt[:, :]))
+    v_w = v(V.tensor_copy(T.w16[HIGH, 0:14], T.wt[:, 2:16]))
     V.wait_ge(S.s, s_v)
     vw()
-    v_r = v(V.tensor_copy(T.row[:, 128:256], T.vwin[:, 0:2048].indirect(T.w16[:, 8:16])))
+    v(V.tensor_copy(T.row[:, 0:128], T.vwin[:, 0:tri + 16].indirect(T.w16[:, 0:8])))
     A.wait_ge(S.v, v_w)
     A.wait_ge(S.s, s_v)
-    s_r = s(A.activation(T.row[:, 0:128], T.vwin[:, 0:2048].indirect(T.w16[:, 0:8]), COPY))
-    for a in range(4):
-        q = slice(32 * a, 32 * a + 32)
-        v(V.tensor_scalar(T.gsc[q, :], T.odd[q, :], -0.75 * 16.0 ** -a, 16.0 ** -a, OP.mult, OP.add))
+    s_r = s(A.activation(T.row[:, 128:256], T.vwin[:, 0:tri + 16].indirect(T.w16[:, 8:16]), COPY))
+    vw()
+    v_t0 = v(V.transpose(T.rt[:, 0:128], T.row[:, 0:128]))
+    V.wait_ge(S.s, s_r)
+    v_t1 = v(V.transpose(T.rt[:, 128:256], T.row[:, 128:256]))
+    at = [0, 256, 448, 576, 640]
+    ne = {}
+    A.wait_ge(S.s, s_r)
+    for b, turned in enumerate((v_t0, v_t0, v_t1, v_t1)):
+        out, rest, entry = T.ne[:, at[b]:at[b + 1]], T.row[:, 64 * b:256], T.rt[:, 64 * b:64 * b + 1]
+        if b % 2 == 0:
+            V.wait_ge(S.v, turned)
+            ne[b] = (S.v, v(V.tensor_scalar(out, rest, entry, None, OP.not_equal)))
+        else:
+            A.wait_ge(S.v, turned)
+            ne[b] = (S.s, s(A.activation(out, rest, ACT.Abs, bias=entry, scale=-1.0)))
+    order = (0, 2, 1, 3)
+    sc = {}
+    for b in order:
+        V.wait_ge(*ne[b])
+        sc[b] = v(V.tensor_tensor_scan(T.sc[:, at[b]:at[b + 1]], T.ne[:, at[b]:at[b + 1]],
+                                       T.vwin[:, tri:tri + 256 - 64 * b], 0.0, OP.min, OP.max))
+    for b in order:
+        V.wait_ge(S.v, sc[b])
+        v(V.tensor_scalar(T.fr[:, 32 * b:32 * b + 32], T.rt[:, 64 * b:64 * b + 32], T.sc[:, at[b + 1] - 1:at[b + 1]],
+                          None, OP.mult))
+    vw()
+    v(V.transpose(T.qf[:, 0:128], T.fr[:, :]))
+    v(V.transpose(T.qf[HIGH, 128:256], T.fr[LOW, :]))
+    v(V.transpose(T.qf[LOW, 128:256], T.fr[HIGH, :]))
 
-    A.wait_ge(S.ps, g_c)
-    for k in (256, 512, 1024):
-        k_s = s(A.activation(T.cwin[:, k:2 * k], T.cwin[:, 0:k], COPY))
-        A.wait_ge(S.s, k_s)
-    s_cr = s(A.activation(T.crow[:, 0:256], T.cwin[:, 0:2048].indirect(T.w16[:, 0:16]), COPY))
     A.wait_ge(S.ldx, 16)
     for t in range(4):
-        s_xs = s(A.activation(T.xs[:, XW * t:XW * t + XW], T.xt[:, t:4 * XW:4], COPY))
+        s(A.activation(T.xs[:, XW * t:XW * t + 128], T.xt[:, t:512:4], COPY))
+        s(A.activation(T.xs[:, XW * t + 128:XW * t + XW:2], T.xt[:, 512 + t:1024:4], COPY))
 
-    V.wait_ge(S.v, v_r)
-    V.wait_ge(S.s, s_r)
-    halves = [slice(64 * h, 64 * h + 64) for h in range(2)]
-    for h in range(2):
-        v(V.transpose(T.rt[halves[h], 0:128], T.row[halves[h], 128 * h:128 * h + 128]))
+    V.wait_ge(S.tc, 8)
     vw()
-    at = [0]
-    for b in range(4):
-        at.append(at[b] + 256 - 32 * b)
-    ne = [v(V.tensor_scalar(T.ne[:, at[b]:at[b + 1]], T.row[:, 32 * b:256], T.rt[:, 32 * b:32 * b + 1], None, OP.not_equal))
-          for b in range(4)]
-    sc = []
-    for b in range(4):
-        V.wait_ge(S.v, ne[b])
-        sc.append(v(V.tensor_tensor_scan(T.sc[:, at[b]:at[b + 1]], T.ne[:, at[b]:at[b + 1]], T.ones[:, 0:256 - 32 * b],
-                                         0.0, OP.mult, OP.add)))
-    for b in range(4):
-        V.wait_ge(S.v, sc[b])
-        v(V.tensor_scalar(T.fr[:, 32 * b:32 * b + 32], T.cst[:, 32 * b:32 * b + 32], T.sc[:, at[b + 1] - 1:at[b + 1]],
-                          T.rt[:, 32 * b:32 * b + 1], OP.is_equal, OP.mult))
+    v(V.tensor_scalar(T.ge[:, :], T.qf[:, 0:256], T.gsc[:, 0:1], 128.0, OP.mult, OP.is_ge))
+    v(V.tensor_scalar(T.gh[:, :], T.qf[:, 0:256], T.gsc[:, 0:1], 512.0, OP.mult, OP.is_ge))
     vw()
-    qf = [v(V.transpose(T.qf[halves[h], 128 * h:128 * h + 128], T.fr[halves[h], 0:128])) for h in range(2)]
-    for h in range(2):
-        V.wait_ge(S.v, qf[h])
-        v(V.tensor_copy(T.qf[halves[1 - h], 128 * h:128 * h + 128], T.qf[halves[h], 128 * h:128 * h + 128]))
-    vw()
-    v(V.tensor_scalar(T.ge[:, :], T.qf[:, :], T.gsc[:, 0:1], 128.0, OP.mult, OP.is_ge))
-    v(V.tensor_scalar(T.gh[:, :], T.qf[:, :], T.gsc[:, 0:1], 512.0, OP.mult, OP.is_ge))
-    vw()
-    v(V.tensor_tensor_scan(T.cc[:, :], T.ge[:, :], T.gh[:, :], 0.0, OP.add, OP.subtract))
+    v_c = v(V.tensor_tensor_scan(T.cc[:, :], T.ge[:, :], T.gh[:, :], 0.0, OP.add, OP.subtract))
     V.wait_ge(S.th, 16)
     vw()
-    le, nn = [], []
-    for k, t in enumerate((T.s0, T.s1)):
-        le.append(v(V.tensor_scalar(T.le[:, 256 * k:256 * k + 256], T.cc[:, :], t[:, 0:1], None, OP.is_le)))
-    for k in range(2):
-        V.wait_ge(S.v, le[k])
-        nn.append(v(V.tensor_tensor_scan(T.nn[:, 256 * k:256 * k + 256], T.ones[:, :], T.le[:, 256 * k:256 * k + 256],
-                                         0.0, OP.mult, OP.add)))
+    v(V.tensor_scalar(T.le[:, :], T.cc[:, :], T.s0[:, 0:1], 2.0, OP.is_le, OP.mult))
+    vw()
+    v(V.tensor_tensor_scan(T.nn[:, :], T.le[:, :], T.vwin[:, tri + 32:tri + 288], -256.0, OP.add, OP.add))
+    A.wait_ge(S.th, 16)
+    A.wait_ge(S.v, v_c)
+    s_n = s(A.activation(T.sg[:, :], T.cc[:, :], ACT.Sign, bias=T.s1[:, 0:1], scale=-1.0, accum_out=T.acc[:, 0:1]))
+    for t in range(4):
+        s_xs = s(A.activation(T.xs[:, XW * t + 129:XW * t + XW:2], T.xt[:, 512 + t:1024:4], COPY))
     V.wait_ge(S.tz, 8)
-    for k in range(2):
-        V.wait_ge(S.v, nn[k])
-        v(V.tensor_scalar(T.jj[:, 2 * k:2 * k + 2], T.z2[:, :], T.nn[:, 256 * k + 255:256 * k + 256], None, OP.add))
-    V.wait_ge(S.tc, 8)
-    V.wait_ge(S.s, s_cr)
+    V.wait_ge(S.s, s_n)
+    v(V.tensor_scalar(T.jj[:, 2:4], T.hf[:, :], T.acc[:, 0:1], 128.0, OP.mult, OP.add))
+    V.wait_ge(S.v, n["v"] - 1)
+    v(V.tensor_scalar(T.jj[:, 0:2], T.hf[:, :], T.nn[:, 255:256], 128.0, OP.mult, OP.add))
     vw()
-    v(V.tensor_copy(T.lg[:, :], T.crow[:, 0:257].indirect(T.jj[:, 0:4])))
-    vw()
-    v(V.transpose(T.lt[:, :], T.lg[:, :]))
+    v(V.tensor_scalar(T.lg[:, :], T.qf[:, 0:272].indirect(T.jj[:, 0:4]), T.gsc[:, 0:1], -128.0, OP.mult, OP.add))
     vw()
     for k in range(2):
-        v_msg = v(V.tensor_copy(T.msg[:, 2 * k:2 * k + 2], T.lt[:, 16 * k:64:32]))
+        v_msg = v(V.transpose(T.lt[:, k:64:2], T.lg[:, 32 * k:32 * k + 32]))
 
     def of(f):
-        return T.msg[:, 2 * (f % 2):2 * (f % 2) + 2]
+        return T.lt[:, 30 + 2 * (f % 2):32 + 2 * (f % 2)]
 
-    def among(f):
-        return 2 * [k for k in plane if k != f].index(r)
+    def to(f, engines):
+        k = 2 * roads(topo, cores, f)[1].index(r)
+        return cores[f], engines, S.la, of(f), T.li[:, k:k + 2]
+    far, near = 2 * (slots[0] % 2), 2 * (r % 2)
     g.wait_ge(S.v, v_msg)
-    g.remote_dma_fused([xfer(topo, core, c, on[4 * i:4 * i + 4], S.rl, of(f), T.rl[:, 0:2])
-                        for i, (c, f, _) in enumerate(road)], local_sem=S.loc)
-    g.remote_dma_fused([xfer(topo, core, cores[f], off[2 * i:2 * i + 2], S.aa, of(f), T.la[:, among(f):among(f) + 2])
-                        for i, f in enumerate(others)], local_sem=S.loc)
-    g.remote_dma(T.rp[:, 0:4], T.msg[:, 0:4], S.rp, S.loc, h_pid, h_rid, mask(on[0:4]))
+    send([(c, on[4 * i:4 * i + 4], S.rl, of(slots[0]), T.rl[:, far:far + 2]) for i, c in enumerate(relays)])
+    send([to(slots[1], off[0:4]), to(slots[3], off[4:8]), (relays[PLACES], on[0:8], S.rp, of(r), T.rl[:, near:near + 2])])
+    send([to(slots[6], off)])
 
+    mq = QUARTERS[r // 2]
+    V.wait_ge(S.v, v_msg)
+    for q in QUARTERS:
+        v(V.tensor_copy(T.oo[q, 14:16], T.lt[mq, 30 + near:32 + near]))
     V.wait_ge(S.ldw, 16)
     v_qw = v(V.quantize_mx(T.qw[:, :], T.pw[:, :], T.wb[:, :]))
-    mq = slice(32 * (r // 2), 32 * (r // 2) + 32)
-    V.wait_ge(S.v, v_msg)
-    for a in range(4):
-        v(V.tensor_copy(T.oa[32 * a:32 * a + 32, 0:2], T.msg[mq, 2 * (r % 2):2 * (r % 2) + 2]))
 
-    def serve(lists, offs, o0, tile, codes, plane8, sem, arrivals):
-        V.wait_ge(sem, arrivals)
-        for a in range(4):
-            v_o = v(V.tensor_copy(offs[32 * a:32 * a + 32, o0:8], lists[mq, :]))
-        vw()
+    V.wait_ge(S.la, 48)
+    for q in QUARTERS:
+        v_o = v(V.tensor_copy(T.oo[q, 0:14], T.li[mq, :]))
+    V.wait_ge(S.s, s_xs)
+    vw()
+    A.wait_ge(S.s, s_xs)
+    A.wait_ge(S.v, v_o)
+    done = []
+    for i, (tile, codes, scales) in enumerate(((T.ta, T.qa, T.pa), (T.tb, T.cb, T.db))):
+        offs = T.oo[:, 8 * i:8 * i + 8]
         for t in range(2):
-            v(V.tensor_copy(tile[:, t:512:4], T.xs[:, XW * t:XW * t + XW].indirect(offs[:, 0:8])))
-        A.wait_ge(S.v, v_o)
+            v(V.tensor_copy(tile[:, t:512:4], T.xs[:, XW * t:XW * t + XW].indirect(offs)))
         for t in range(2, 4):
-            s_t = s(A.activation(tile[:, t:512:4], T.xs[:, XW * t:XW * t + XW].indirect(offs[:, 0:8]), COPY))
+            s_t = s(A.activation(tile[:, t:512:4], T.xs[:, XW * t:XW * t + XW].indirect(offs), COPY))
         vw()
         V.wait_ge(S.s, s_t)
-        return v(V.quantize_mx(codes[:, :], plane8[:, :], tile[:, :]))
+        done.append(v(V.quantize_mx(codes[:, 0:128], scales[:, 0:128], tile[:, :])))
 
-    V.wait_ge(S.s, s_xs)
-    A.wait_ge(S.s, s_xs)
-    v_qa = serve(T.la, T.oa, 2, T.ta, T.qa, T.pa, S.aa, 6)
-    v_qb = serve(T.lb, T.ob, 0, T.tb, T.qb, T.pb, S.ab, 32)
-
-    def codes(q, i):
-        return u8(q[:, 32 * i:32 * i + 32])
-
-    def scales(p, i):
-        return p[:, 32 * i:32 * i + 32]
-    for done, first, view, src, dst, sem in ((v_qa, 1, codes, T.qa, T.ra, S.ra), (v_qa, 1, scales, T.pa, T.rz, S.rz),
-                                             (v_qb, 0, codes, T.qb, T.rc, S.rc), (v_qb, 0, scales, T.pb, T.rs, S.rs)):
-        g.wait_ge(S.v, done)
-        g.remote_dma_fused([xfer(topo, core, road[h][0], on[4 * h:4 * h + 4], sem, view(src, h), view(dst, 0))
-                            for h in range(first, 4)], local_sem=S.loc)
-    g.wait_ge(S.loc, 16 + 16 + 6 + 4 + 2 * 12 + 2 * 16)
-    here = slice(32 * me, 32 * me + 32)
-    D.wait_ge(S.v, v_qa)
-    D.dma_start(u8(T.ca[:, here]), u8(T.qa[:, 0:32])).then_inc(S.own, 16)
-    D.dma_start(T.da[:, here], T.pa[:, 0:32]).then_inc(S.own, 16)
+    for i, (codes, scales) in enumerate(((T.qa, T.pa), (T.cb, T.db))):
+        g.wait_ge(S.v, done[i])
+        w = 32 * len(RUNS[2 * i])
+        send([(relays[2 * i + k], on[8 * k:8 * k + 8], S.rc, u8(codes[:, w * k:w * k + w]), u8(T.rc[:, 0:w])) for k in range(2)])
+        send([(relays[2 * i + k], on[8 * k:8 * k + 8], S.rs, scales[:, w * k:w * k + w], T.rs[:, 0:w]) for k in range(2)])
+    there = landing(T, 6)
+    send([(cores[slots[6]], off, S.ad, u8(T.cb[:, 64:96]), u8(there[0]))])
+    send([(cores[slots[6]], off, S.ad, T.db[:, 64:96], there[1])])
+    g.wait_ge(S.loc, n["loc"])
 
     P.wait_ge(S.v, v_qw)
-    P.wait_ge(S.ac, 48)
-    P.wait_ge(S.own, 32)
+    P.wait_ge(S.ac, 32)
     P.matmul_mx(T.m0[:, 0:128], T.qw[:, :], T.pw[:, :], T.ca[:, :], T.da[:, :], True, True).then_inc(S.te, 1)
-    P.wait_ge(S.ad, 64)
-    P.matmul_mx(T.m1[:, 0:128], T.qw[:, :], T.pw[:, :], T.cb[:, :], T.db[:, :], True, True).then_inc(S.te, 1)
+    P.wait_ge(S.v, done[1])
+    P.wait_ge(S.ad, 48)
+    P.matmul_mx(T.m1[:, 0:128], T.qw[:, :], T.pw[:, :], T.cb[:, 96:224], T.db[:, 96:224], True, True).then_inc(S.te, 1)
     A.wait_ge(S.te, 1)
     s_y = s(A.activation(T.ys[:, 0:128], T.m0[:, 0:128], COPY))
     V.wait_ge(S.oy, 8)

@@ -9,11 +9,12 @@ PO = 32 + XW
 SMALL = {"allow_small_or_imprecise_dtypes": True}
 
 SCRATCH = {"wt": ("sbuf", [64, 16], "int32"), "hw": ("dram", [128, 2], "int32"),
+           "ne": ("sbuf", [128, 4, 288], "bfloat16"), "sc": ("sbuf", [128, 4, 288], "bfloat16"),
            "m0": ("psum", [128, 512], "float32"), "m1": ("psum", [128, 512], "float32")}
 for _t, _b in (("int32", "pi 1 pm 1 w0 2 ec 16 eq 16"),
                ("uint16", "w16 16 w2 32 jj 4 oo 16 ou 4 oy 16"),
                ("float32", "acc 1 e1 16 e2 16 e3 16 e4 16 b1 4 b2 4 b3 4 ys 256 yo 256"),
-               ("bfloat16", "k0 2 hf 2 s0 1 s1 1 gsc 1 vwin 2336 pos %d row 256 rt 256 ne 640 sc 640 fr 128 qf 272 "
+               ("bfloat16", "k0 2 hf 2 s0 1 s1 1 gsc 1 vwin 2064 pos %d row 256 rt 256 cm 32 td 768 qf 272 "
                             "ge 256 gh 256 cc 256 le 256 nn 256 sg 256 lg 64 lt 64 li 14 rl 4 xt 1024 xs %d "
                             "wb 512 ta 512 tb 512 vp 64 pr 512 pt 512 p2 16 p3 16" % (8 * PO, 4 * XW)),
                ("float8_e4m3fn_x4", "qw 128 qa 128 ca 128 cb 224 rc 64"),
@@ -231,67 +232,61 @@ def rank_program(g, core, T, topo):
     D.dma_start(T.xt[:, :], T.x[:, :]).then_inc(S.ldx, 16)
     D.dma_start(T.wb[:, :], T.w[:, :]).then_inc(S.ldw, 16)
 
-    tri = 2048
+    none = 2048
     g_v = ps(g.iota(T.vwin[:, 0:128], [[1, 128]], 128, 0, **SMALL))
-    v_z = v(V.memset(T.vwin[:, tri:tri + 288], 0.0))
+    v_z = v(V.memset(T.cm[:, :], -1.0))
     g.wait_ge(S.v, v_z)
     g.wait_ge(S.ps, g_v)
-    for q in QUARTERS[0:2]:
-        g_t = ps(g.affine_select(T.vwin[q, tri:tri + 32], T.vwin[q, tri:tri + 32], [[-1, 32]], OP.not_equal, 1.0, 0, 1))
+    for q in QUARTERS:
+        g_t = ps(g.affine_select(T.cm[q, :], T.cm[q, :], [[-1, 32]], OP.not_equal, 0.0, 0, 1))
     g.wait_ge(S.ld0, 16)
     send([(relays[PLACES], on, S.hs, T.w0[:, 0:2], T.hw[:, :])])
 
+    v(V.memset(T.vwin[:, none:none + 16], 0.0))
     v(V.memset(T.qf[:, 256:272], 0.0))
-    v(V.memset(T.w16[HIGH, 14:16], tri))
+    v(V.memset(T.w16[HIGH, 14:16], none))
+    v(V.memset(T.ne[:, :, 256:288], 1.0))
     V.wait_ge(S.ps, g_v)
-    for k, f in ((128, 2.0), (256, 4.0)):
-        v_v = v(V.tensor_scalar(T.vwin[:, k:2 * k], T.vwin[:, 0:k], f, None, OP.mult))
-        vw()
-    v(V.tensor_scalar(T.vwin[:, 512:1024], T.vwin[:, 0:512], 16.0, None, OP.mult))
-    v(V.tensor_scalar(T.vwin[:, 1024:1536], T.vwin[:, 0:512], 256.0, None, OP.mult))
-    A.wait_ge(S.v, v_v)
-    s_v = s(A.activation(T.vwin[:, 1536:2048], T.vwin[:, 0:512], COPY, scale=4096.0))
-    V.wait_ge(S.ps, g_t)
-    v(V.tensor_copy(T.vwin[HIGH, tri:tri + 32], T.vwin[LOW, tri:tri + 32]))
+    A.wait_ge(S.ps, g_v)
+    for e in range(1, 16):
+        if e <= 10:
+            v(V.tensor_scalar(T.vwin[:, 128 * e:128 * e + 128], T.vwin[:, 0:128], 2.0 ** e, None, OP.mult))
+        else:
+            s_v = s(A.activation(T.vwin[:, 128 * e:128 * e + 128], T.vwin[:, 0:128], COPY, scale=2.0 ** e))
 
     V.wait_ge(S.ld, 64)
     v(V.tensor_copy(T.w16[LOW, :], T.wt[:, :]))
     v_w = v(V.tensor_copy(T.w16[HIGH, 0:14], T.wt[:, 2:16]))
+    v(V.memset(T.td[:, 0:384], 0.0))
     V.wait_ge(S.s, s_v)
-    vw()
-    v(V.tensor_copy(T.row[:, 0:128], T.vwin[:, 0:tri + 16].indirect(T.w16[:, 0:8])))
+    V.wait_ge(S.v, v_w)
+    v_r = v(V.tensor_copy(T.row[:, 0:128], T.vwin[:, 0:none + 16].indirect(T.w16[:, 0:8])))
+    v(V.memset(T.td[:, 384:768], 0.0))
     A.wait_ge(S.v, v_w)
     A.wait_ge(S.s, s_v)
-    s_r = s(A.activation(T.row[:, 128:256], T.vwin[:, 0:tri + 16].indirect(T.w16[:, 8:16]), COPY))
-    vw()
+    s_r = s(A.activation(T.row[:, 128:256], T.vwin[:, 0:none + 16].indirect(T.w16[:, 8:16]), COPY))
+    V.wait_ge(S.v, v_r)
     v_t0 = v(V.transpose(T.rt[:, 0:128], T.row[:, 0:128]))
     V.wait_ge(S.s, s_r)
     v_t1 = v(V.transpose(T.rt[:, 128:256], T.row[:, 128:256]))
-    at = [0, 256, 448, 576, 640]
-    ne = {}
-    A.wait_ge(S.s, s_r)
+    at = [0, 288, 512, 672]
+    ne, td = [], []
+    A.wait_ge(S.ps, g_t)
     for b, turned in enumerate((v_t0, v_t0, v_t1, v_t1)):
-        out, rest, entry = T.ne[:, at[b]:at[b + 1]], T.row[:, 64 * b:256], T.rt[:, 64 * b:64 * b + 1]
-        if b % 2 == 0:
-            V.wait_ge(S.v, turned)
-            ne[b] = (S.v, v(V.tensor_scalar(out, rest, entry, None, OP.not_equal)))
-        else:
-            A.wait_ge(S.v, turned)
-            ne[b] = (S.s, s(A.activation(out, rest, ACT.Abs, bias=entry, scale=-1.0)))
-    order = (0, 2, 1, 3)
-    sc = {}
-    for b in order:
-        V.wait_ge(*ne[b])
-        sc[b] = v(V.tensor_tensor_scan(T.sc[:, at[b]:at[b + 1]], T.ne[:, at[b]:at[b + 1]],
-                                       T.vwin[:, tri:tri + 256 - 64 * b], 0.0, OP.min, OP.max))
-    for b in order:
-        V.wait_ge(S.v, sc[b])
-        v(V.tensor_scalar(T.fr[:, 32 * b:32 * b + 32], T.rt[:, 64 * b:64 * b + 32], T.sc[:, at[b + 1] - 1:at[b + 1]],
-                          None, OP.mult))
+        entry = T.rt[:, 64 * b:64 * b + 1]
+        V.wait_ge(S.v, turned)
+        ne.append(v(V.tensor_scalar(T.ne[:, b, 64 * b:256], T.row[:, 64 * b:256], entry, None, OP.not_equal)))
+        A.wait_ge(S.v, turned)
+        td.append(s(A.activation(T.td[:, at[b]:at[b] + 32], T.cm[:, :], ACT.Relu, bias=entry, scale=2.0 ** 30)))
+    for b in range(4):
+        V.wait_ge(S.v, ne[b])
+        V.wait_ge(S.s, td[b])
+        v(V.tensor_tensor_scan(T.sc[:, b, 64 * b:287], T.ne[:, b, 64 * b:287], T.td[:, at[b]:at[b] + 287 - 64 * b],
+                               0.0, OP.mult, OP.add))
     vw()
-    v(V.transpose(T.qf[:, 0:128], T.fr[:, :]))
-    v(V.transpose(T.qf[HIGH, 128:256], T.fr[LOW, :]))
-    v(V.transpose(T.qf[LOW, 128:256], T.fr[HIGH, :]))
+    v(V.transpose(T.qf[:, 0:128], T.sc[:, :, 255:287]))
+    v(V.transpose(T.qf[HIGH, 128:256], T.sc[LOW, :, 255:287]))
+    v(V.transpose(T.qf[LOW, 128:256], T.sc[HIGH, :, 255:287]))
 
     A.wait_ge(S.ldx, 16)
     for t in range(4):
@@ -308,7 +303,7 @@ def rank_program(g, core, T, topo):
     vw()
     v(V.tensor_scalar(T.le[:, :], T.cc[:, :], T.s0[:, 0:1], 2.0, OP.is_le, OP.mult))
     vw()
-    v(V.tensor_tensor_scan(T.nn[:, :], T.le[:, :], T.vwin[:, tri + 32:tri + 288], -256.0, OP.add, OP.add))
+    v(V.tensor_tensor_scan(T.nn[:, :], T.le[:, :], T.td[:, 32:288], -256.0, OP.add, OP.add))
     A.wait_ge(S.th, 16)
     A.wait_ge(S.v, v_c)
     s_n = s(A.activation(T.sg[:, :], T.cc[:, :], ACT.Sign, bias=T.s1[:, 0:1], scale=-1.0, accum_out=T.acc[:, 0:1]))
@@ -351,16 +346,19 @@ def rank_program(g, core, T, topo):
     vw()
     A.wait_ge(S.s, s_xs)
     A.wait_ge(S.v, v_o)
-    done = []
-    for i, (tile, codes, scales) in enumerate(((T.ta, T.qa, T.pa), (T.tb, T.cb, T.db))):
-        offs = T.oo[:, 8 * i:8 * i + 8]
-        for t in range(2):
-            v(V.tensor_copy(tile[:, t:512:4], T.xs[:, XW * t:XW * t + XW].indirect(offs)))
-        for t in range(2, 4):
-            s_t = s(A.activation(tile[:, t:512:4], T.xs[:, XW * t:XW * t + XW].indirect(offs), COPY))
-        vw()
-        V.wait_ge(S.s, s_t)
-        done.append(v(V.quantize_mx(codes[:, 0:128], scales[:, 0:128], tile[:, :])))
+    tiles = ((T.ta, T.qa, T.pa), (T.tb, T.cb, T.db))
+
+    def pick(i, t):
+        return tiles[i][0][:, t:512:4], T.xs[:, XW * t:XW * t + XW].indirect(T.oo[:, 8 * i:8 * i + 8])
+
+    def pack(i, v_t):
+        V.wait_ge(S.v, v_t)
+        V.wait_ge(S.s, s_t[2 * i + 1])
+        return v(V.quantize_mx(tiles[i][1][:, 0:128], tiles[i][2][:, 0:128], tiles[i][0][:, :]))
+    s_t = [s(A.activation(*pick(i, t), COPY)) for i in range(2) for t in (2, 3)]
+    v_t = [v(V.tensor_copy(*pick(i, t))) for i, t in ((0, 0), (0, 1), (1, 0))]
+    done = [pack(0, v_t[1])]
+    done.append(pack(1, v(V.tensor_copy(*pick(1, 1)))))
 
     for i, (codes, scales) in enumerate(((T.qa, T.pa), (T.cb, T.db))):
         g.wait_ge(S.v, done[i])

@@ -15,14 +15,14 @@ for _t, _b in (("int32", "pi 1 pm 1 w0 2 ec 16 eq 16"),
                ("uint16", "w16 16 w2 32 jj 4 oo 16 ou 4 oy 16"),
                ("float32", "acc 1 e1 16 e2 16 e3 16 e4 16 b1 4 b2 4 b3 4 ys 256 yo 256"),
                ("bfloat16", "k0 2 hf 2 s0 1 s1 1 gsc 1 vwin 2064 pos %d row 256 rt 256 cm 32 td 768 qf 272 "
-                            "ge 256 gh 256 cc 256 le 256 nn 256 sg 256 lg 64 lt 64 li 14 rl 4 xt 1024 xs %d "
+                            "ge 256 gh 256 cc 256 le 256 nn 256 sg 256 lg 64 lt 64 li 16 rl 4 xt 1024 xs %d "
                             "wb 512 ta 512 tb 512 vp 64 pr 512 pt 512 p2 16 p3 16" % (8 * PO, 4 * XW)),
-               ("float8_e4m3fn_x4", "qw 128 qa 128 ca 128 cb 224 rc 64"),
-               ("uint8", "pw 128 pa 128 da 128 db 224 rs 64")):
+               ("float8_e4m3fn_x4", "qw 128 qa 128 ca 128 cb 224 rc 128"),
+               ("uint8", "pw 128 pa 128 da 128 db 224 rs 128")):
     _w = _b.split()
     for _i in range(0, len(_w), 2):
         SCRATCH[_w[_i]] = ("sbuf", [128, int(_w[_i + 1])], _t)
-SEMAPHORES = "ld ldx ldw ld0 v s ps te la ac ad st su loc rl rp rc rs th tz tc hs oy".split()
+SEMAPHORES = "ld ldx ldw ld0 v s ps te la lb ac ad st su loc rl rp th tz tc hs oy j0 j1 j2 j3 j4 j5 j6 j7 j8 j9".split()
 QUARTERS = [slice(32 * a, 32 * a + 32) for a in range(4)]
 LOW, HIGH = slice(0, 64), slice(64, 128)
 
@@ -41,11 +41,17 @@ def roads(topo, cores, r):
     a = mine.index(r)
     f = [far[(h - a) % 4] for h in range(4)]
     m = [mine[(a + j) % 4] for j in range(4)]
-    return [same[0], other[0], same[1], other[1]], [f[0], m[1], f[1], m[2], f[2], f[3], m[3], r]
+    return [same[0], other[0], same[1], other[1]], f + m[1:] + [r]
 
 
-RUNS = ((0, 1), (2, 3), (4,), (5,))
 PLACES = 2
+JOBS = ((0, 0, (4, 5)), (1, 0, (6,)), (3, 1, (4, 5)), (1, 1, (6,)),
+        (0, 0, (0, 1)), (1, 0, (2, 3)), (2, 1, (0, 1)), (3, 1, (2, 3)))
+CALLS = ((0,), (1,), (2,), (3,), (4, 5), (6, 7))
+
+
+def width(i):
+    return 4 if any(i in c and len(c) == 4 for c in CALLS) else 8
 
 
 def mask(engines):
@@ -70,6 +76,12 @@ def landing(T, run):
     return T.cb[:, at], T.db[:, at], T.sem.ad
 
 
+def stop(T, i, j=None):
+    part, runs = JOBS[i][1:]
+    a = 64 * (runs[0] // 4)
+    return (T.rc, T.rs)[part][:, a:a + 32 * len(runs)] if j is None else (T.rc, T.rs)[part][:, a + 32 * j:a + 32 * j + 32]
+
+
 def column(run):
     return 32 * run if run < 4 else 128 + 32 * ((run - 3) % 4 if run < 7 else 0)
 
@@ -77,7 +89,7 @@ def column(run):
 def relay(g, core, T, topo, r, h):
     cores = T.cores
     slots = roads(topo, cores, r)[1]
-    f = slots[RUNS[h][0]]
+    f = slots[h]
     en = topo.engines(core, cores[f])
     V, A, D, S = g.vector, g.scalar, g.sync, T.sem
     n = [0]
@@ -143,7 +155,7 @@ def relay(g, core, T, topo, r, h):
         for half in (LOW, HIGH):
             for k in range(2):
                 v(V.tensor_copy(T.w2[half, k:32:2], T.e4[LOW, :]))
-        V.wait_ge(S.rl, 4)
+        V.wait_ge(S.rl, 8)
         V.wait_ge(S.rp, 8)
         vw()
         for k in range(4):
@@ -166,20 +178,25 @@ def relay(g, core, T, topo, r, h):
         for q in QUARTERS:
             v(V.tensor_copy(T.oy[q, :], T.p3[QUARTERS[0], :]))
 
-    at = 2 * roads(topo, cores, f)[1].index(r)
-    g.wait_ge(S.rl, 4)
-    send(f, S.la, T.rl[:, 2 * (f % 2):2 * (f % 2) + 2], T.li[:, at:at + 2])
+    if h % 2 == 0:
+        g.wait_ge(S.rl, 8)
+        at = [2 * roads(topo, cores, k)[1].index(r) for k in slots[h:h + 2]]
+        g.remote_dma_fused([xfer(topo, core, cores[k], en[4 * i:4 * i + 4], S.la, T.rl[:, 2 * (f % 2):2 * (f % 2) + 2],
+                                 T.li[:, at[i]:at[i] + 2]) for i, k in enumerate(slots[h:h + 2])], local_sem=S.loc)
+        left[0] += len(en)
     if h == PLACES:
         g.wait_ge(S.rp, 8)
         g.wait_ge(S.v, n[0])
         send(r, S.oy, T.oy[:, 0:16], T.oy[:, 0:16])
-    share = len(en) // len(RUNS[h])
-    for part, (sem, buf, view) in enumerate(((S.rc, T.rc, u8), (S.rs, T.rs, lambda a: a))):
-        g.wait_ge(sem, 8)
-        g.remote_dma_fused([xfer(topo, core, cores[slots[run]], en[share * i:share * i + share], landing(T, run)[2],
-                                 view(buf[:, 32 * i:32 * i + 32]), view(landing(T, run)[part]))
-                            for i, run in enumerate(RUNS[h])], local_sem=S.loc)
-        left[0] += len(en)
+    for i, (k, part, runs) in enumerate(JOBS):
+        if k == h:
+            view = (u8, lambda a: a)[part]
+            share = len(en) // len(runs)
+            g.wait_ge(S["j%d" % i], width(i))
+            g.remote_dma_fused([xfer(topo, core, cores[slots[run]], en[share * j:share * j + share], landing(T, run)[2],
+                                     view(stop(T, i, j)), view(landing(T, run)[part]))
+                                for j, run in enumerate(runs)], local_sem=S.loc)
+            left[0] += len(en)
     g.wait_ge(S.loc, left[0])
 
 
@@ -234,10 +251,10 @@ def rank_program(g, core, T, topo):
 
     none = 2048
     g_v = ps(g.iota(T.vwin[:, 0:128], [[1, 128]], 128, 0, **SMALL))
-    v_z = v(V.memset(T.cm[:, :], -1.0))
+    v_z = v(V.memset(T.cm[LOW, :], -1.0))
     g.wait_ge(S.v, v_z)
     g.wait_ge(S.ps, g_v)
-    for q in QUARTERS:
+    for q in QUARTERS[0:2]:
         g_t = ps(g.affine_select(T.cm[q, :], T.cm[q, :], [[-1, 32]], OP.not_equal, 0.0, 0, 1))
     g.wait_ge(S.ld0, 16)
     send([(relays[PLACES], on, S.hs, T.w0[:, 0:2], T.hw[:, :])])
@@ -265,13 +282,15 @@ def rank_program(g, core, T, topo):
     A.wait_ge(S.v, v_w)
     A.wait_ge(S.s, s_v)
     s_r = s(A.activation(T.row[:, 128:256], T.vwin[:, 0:none + 16].indirect(T.w16[:, 8:16]), COPY))
+    A.wait_ge(S.ps, g_t)
+    s_m = s(A.activation(T.cm[HIGH, :], T.cm[LOW, :], COPY))
     V.wait_ge(S.v, v_r)
     v_t0 = v(V.transpose(T.rt[:, 0:128], T.row[:, 0:128]))
     V.wait_ge(S.s, s_r)
     v_t1 = v(V.transpose(T.rt[:, 128:256], T.row[:, 128:256]))
+    A.wait_ge(S.s, s_m)
     at = [0, 288, 512, 672]
     ne, td = [], []
-    A.wait_ge(S.ps, g_t)
     for b, turned in enumerate((v_t0, v_t0, v_t1, v_t1)):
         entry = T.rt[:, 64 * b:64 * b + 1]
         V.wait_ge(S.v, turned)
@@ -284,104 +303,119 @@ def rank_program(g, core, T, topo):
         v(V.tensor_tensor_scan(T.sc[:, b, 64 * b:287], T.ne[:, b, 64 * b:287], T.td[:, at[b]:at[b] + 287 - 64 * b],
                                0.0, OP.mult, OP.add))
     vw()
-    v(V.transpose(T.qf[:, 0:128], T.sc[:, :, 255:287]))
+    turned = [v(V.transpose(T.qf[:, 0:128], T.sc[:, :, 255:287]))]
     v(V.transpose(T.qf[HIGH, 128:256], T.sc[LOW, :, 255:287]))
-    v(V.transpose(T.qf[LOW, 128:256], T.sc[HIGH, :, 255:287]))
+    turned.append(v(V.transpose(T.qf[LOW, 128:256], T.sc[HIGH, :, 255:287])))
 
     A.wait_ge(S.ldx, 16)
     for t in range(4):
-        s(A.activation(T.xs[:, XW * t:XW * t + 128], T.xt[:, t:512:4], COPY))
-        s(A.activation(T.xs[:, XW * t + 128:XW * t + XW:2], T.xt[:, 512 + t:1024:4], COPY))
+        s_xs = s(A.activation(T.xs[:, XW * t:XW * t + 128], T.xt[:, t:512:4], COPY))
+
+    def upper(t):
+        for k in range(2):
+            v(V.tensor_copy(T.xs[:, XW * t + 128 + k:XW * t + XW:2], T.xt[:, 512 + t:1024:4]))
 
     V.wait_ge(S.tc, 8)
-    vw()
-    v(V.tensor_scalar(T.ge[:, :], T.qf[:, 0:256], T.gsc[:, 0:1], 128.0, OP.mult, OP.is_ge))
-    v(V.tensor_scalar(T.gh[:, :], T.qf[:, 0:256], T.gsc[:, 0:1], 512.0, OP.mult, OP.is_ge))
+    parts = (slice(0, 128), slice(128, 256))
+    for k, part in enumerate(parts):
+        V.wait_ge(S.v, turned[k])
+        v(V.tensor_scalar(T.ge[:, part], T.qf[:, part], T.gsc[:, 0:1], 128.0, OP.mult, OP.is_ge))
+        v(V.tensor_scalar(T.gh[:, part], T.qf[:, part], T.gsc[:, 0:1], 512.0, OP.mult, OP.is_ge))
     vw()
     v_c = v(V.tensor_tensor_scan(T.cc[:, :], T.ge[:, :], T.gh[:, :], 0.0, OP.add, OP.subtract))
+    V.wait_ge(S.ldx, 16)
+    upper(0)
     V.wait_ge(S.th, 16)
-    vw()
-    v(V.tensor_scalar(T.le[:, :], T.cc[:, :], T.s0[:, 0:1], 2.0, OP.is_le, OP.mult))
-    vw()
-    v(V.tensor_tensor_scan(T.nn[:, :], T.le[:, :], T.td[:, 32:288], -256.0, OP.add, OP.add))
+    V.wait_ge(S.v, v_c)
+    le = [v(V.tensor_scalar(T.le[:, part], T.cc[:, part], T.s0[:, 0:1], None, OP.is_le)) for part in parts]
+    for k, part in enumerate(parts):
+        V.wait_ge(S.v, le[k])
+        v(V.tensor_tensor_scan(T.nn[:, part], T.le[:, part], T.td[:, 32:160], 0.0, OP.add, OP.add))
     A.wait_ge(S.th, 16)
     A.wait_ge(S.v, v_c)
     s_n = s(A.activation(T.sg[:, :], T.cc[:, :], ACT.Sign, bias=T.s1[:, 0:1], scale=-1.0, accum_out=T.acc[:, 0:1]))
-    for t in range(4):
-        s_xs = s(A.activation(T.xs[:, XW * t + 129:XW * t + XW:2], T.xt[:, 512 + t:1024:4], COPY))
     V.wait_ge(S.tz, 8)
     V.wait_ge(S.s, s_n)
     v(V.tensor_scalar(T.jj[:, 2:4], T.hf[:, :], T.acc[:, 0:1], 128.0, OP.mult, OP.add))
     V.wait_ge(S.v, n["v"] - 1)
-    v(V.tensor_scalar(T.jj[:, 0:2], T.hf[:, :], T.nn[:, 255:256], 128.0, OP.mult, OP.add))
-    vw()
+    v(V.tensor_scalar(T.jj[:, 0:2], T.td[:, 32:34], T.nn[:, 127:128], T.nn[:, 255:256], OP.add, OP.add))
+    upper(1)
+    V.wait_ge(S.v, n["v"] - 2)
     v(V.tensor_scalar(T.lg[:, :], T.qf[:, 0:272].indirect(T.jj[:, 0:4]), T.gsc[:, 0:1], -128.0, OP.mult, OP.add))
-    vw()
+    upper(2)
+    V.wait_ge(S.v, n["v"] - 2)
     for k in range(2):
         v_msg = v(V.transpose(T.lt[:, k:64:2], T.lg[:, 32 * k:32 * k + 32]))
+    upper(3)
 
     def of(f):
         return T.lt[:, 30 + 2 * (f % 2):32 + 2 * (f % 2)]
 
     def to(f, engines):
         k = 2 * roads(topo, cores, f)[1].index(r)
-        return cores[f], engines, S.la, of(f), T.li[:, k:k + 2]
+        return cores[f], engines, S.lb, of(f), T.li[:, k:k + 2]
     far, near = 2 * (slots[0] % 2), 2 * (r % 2)
     g.wait_ge(S.v, v_msg)
-    send([(c, on[4 * i:4 * i + 4], S.rl, of(slots[0]), T.rl[:, far:far + 2]) for i, c in enumerate(relays)])
-    send([to(slots[1], off[0:4]), to(slots[3], off[4:8]), (relays[PLACES], on[0:8], S.rp, of(r), T.rl[:, near:near + 2])])
+    send([(c, on[8 * i:8 * i + 8], S.rl, of(slots[0]), T.rl[:, far:far + 2]) for i, c in enumerate(relays[0::2])])
+    send([to(slots[4], off[0:4]), to(slots[5], off[4:8]), (relays[PLACES], on[0:8], S.rp, of(r), T.rl[:, near:near + 2])])
     send([to(slots[6], off)])
 
     mq = QUARTERS[r // 2]
+
+    def spread(a, b, lists):
+        return [v(V.tensor_copy(T.oo[q, 2 * a:2 * b], lists)) for q in QUARTERS][-1]
+
+    def gather(a, b, ready):
+        tile = (T.ta, T.tb)[a // 4]
+        sides = [(tile[:, 128 * (a % 4) + t:128 * ((b - 1) % 4 + 1):4],
+                  T.xs[:, XW * t:XW * t + XW].indirect(T.oo[:, 2 * a:2 * b])) for t in range(4)]
+        V.wait_ge(S.v, ready)
+        A.wait_ge(S.v, ready)
+        return [v(V.tensor_copy(*x)) for x in sides[0:2]][-1], [s(A.activation(*x, COPY)) for x in sides[2:4]][-1]
+
+    def pack(codes, scales, tile, made):
+        V.wait_ge(S.v, made[0])
+        V.wait_ge(S.s, made[1])
+        return v(V.quantize_mx(codes[:, 0:128], scales[:, 0:128], tile[:, :]))
     V.wait_ge(S.v, v_msg)
-    for q in QUARTERS:
-        v(V.tensor_copy(T.oo[q, 14:16], T.lt[mq, 30 + near:32 + near]))
+    v_o = spread(7, 8, T.lt[mq, 30 + near:32 + near])
     V.wait_ge(S.ldw, 16)
     v_qw = v(V.quantize_mx(T.qw[:, :], T.pw[:, :], T.wb[:, :]))
-
-    V.wait_ge(S.la, 48)
-    for q in QUARTERS:
-        v_o = v(V.tensor_copy(T.oo[q, 0:14], T.li[mq, :]))
     V.wait_ge(S.s, s_xs)
-    vw()
     A.wait_ge(S.s, s_xs)
-    A.wait_ge(S.v, v_o)
-    tiles = ((T.ta, T.qa, T.pa), (T.tb, T.cb, T.db))
+    gather(7, 8, v_o)
+    V.wait_ge(S.lb, 16)
+    made = gather(4, 7, spread(4, 7, T.li[mq, 8:14]))
+    V.wait_ge(S.la, 16)
+    v_o = spread(0, 4, T.li[mq, 0:8])
+    v_near = pack(T.cb, T.db, T.tb, made)
+    v_far = pack(T.qa, T.pa, T.ta, gather(0, 4, v_o))
 
-    def pick(i, t):
-        return tiles[i][0][:, t:512:4], T.xs[:, XW * t:XW * t + XW].indirect(T.oo[:, 8 * i:8 * i + 8])
+    g.wait_ge(S.v, v_near)
 
-    def pack(i, v_t):
-        V.wait_ge(S.v, v_t)
-        V.wait_ge(S.s, s_t[2 * i + 1])
-        return v(V.quantize_mx(tiles[i][1][:, 0:128], tiles[i][2][:, 0:128], tiles[i][0][:, :]))
-    s_t = [s(A.activation(*pick(i, t), COPY)) for i in range(2) for t in (2, 3)]
-    v_t = [v(V.tensor_copy(*pick(i, t))) for i, t in ((0, 0), (0, 1), (1, 0))]
-    done = [pack(0, v_t[1])]
-    done.append(pack(1, v(V.tensor_copy(*pick(1, 1)))))
-
-    for i, (codes, scales) in enumerate(((T.qa, T.pa), (T.cb, T.db))):
-        g.wait_ge(S.v, done[i])
-        w = 32 * len(RUNS[2 * i])
-        send([(relays[2 * i + k], on[8 * k:8 * k + 8], S.rc, u8(codes[:, w * k:w * k + w]), u8(T.rc[:, 0:w])) for k in range(2)])
-        send([(relays[2 * i + k], on[8 * k:8 * k + 8], S.rs, scales[:, w * k:w * k + w], T.rs[:, 0:w]) for k in range(2)])
-    there = landing(T, 6)
-    send([(cores[slots[6]], off, S.ad, u8(T.cb[:, 64:96]), u8(there[0]))])
-    send([(cores[slots[6]], off, S.ad, T.db[:, 64:96], there[1])])
+    def job(i):
+        h, part, runs = JOBS[i]
+        src = ((T.qa, T.cb), (T.pa, T.db))[part][runs[0] // 4][:, 32 * (runs[0] % 4):32 * (runs[-1] % 4 + 1)]
+        view = (u8, lambda a: a)[part]
+        k = width(i) * (i % (16 // width(i)))
+        return relays[h], on[k:k + width(i)], S["j%d" % i], view(src), view(stop(T, i))
+    for call in CALLS:
+        if JOBS[call[0]][2][0] < 4:
+            g.wait_ge(S.v, v_far)
+        send([job(i) for i in call])
     g.wait_ge(S.loc, n["loc"])
 
-    P.wait_ge(S.v, v_qw)
-    P.wait_ge(S.ac, 32)
-    P.matmul_mx(T.m0[:, 0:128], T.qw[:, :], T.pw[:, :], T.ca[:, :], T.da[:, :], True, True).then_inc(S.te, 1)
-    P.wait_ge(S.v, done[1])
-    P.wait_ge(S.ad, 48)
+    P.wait_ge(S.v, v_near)
+    P.wait_ge(S.ad, 32)
     P.matmul_mx(T.m1[:, 0:128], T.qw[:, :], T.pw[:, :], T.cb[:, 96:224], T.db[:, 96:224], True, True).then_inc(S.te, 1)
+    P.wait_ge(S.ac, 8 * sum(runs[0] < 4 for _, _, runs in JOBS))
+    P.matmul_mx(T.m0[:, 0:128], T.qw[:, :], T.pw[:, :], T.ca[:, :], T.da[:, :], True, True).then_inc(S.te, 1)
     A.wait_ge(S.te, 1)
-    s_y = s(A.activation(T.ys[:, 0:128], T.m0[:, 0:128], COPY))
+    s_y = s(A.activation(T.ys[:, 128:256], T.m1[:, 0:128], COPY))
     V.wait_ge(S.oy, 8)
     A.wait_ge(S.oy, 8)
     V.wait_ge(S.te, 2)
-    v_y = v(V.tensor_copy(T.ys[:, 128:256], T.m1[:, 0:128]))
+    v_y = v(V.tensor_copy(T.ys[:, 0:128], T.m0[:, 0:128]))
     vw()
     V.wait_ge(S.s, s_y)
     v_o = v(V.tensor_copy(T.yo[:, 0:128], T.ys[:, 0:256].indirect(T.oy[:, 0:8])))

@@ -10,19 +10,20 @@ SMALL = {"allow_small_or_imprecise_dtypes": True}
 
 SCRATCH = {"wt": ("sbuf", [64, 16], "int32"), "hw": ("dram", [128, 2], "int32"),
            "ne": ("sbuf", [128, 4, 288], "bfloat16"), "sc": ("sbuf", [128, 4, 288], "bfloat16"),
-           "m0": ("psum", [128, 512], "float32"), "m1": ("psum", [128, 512], "float32")}
+           "m0": ("psum", [128, 512], "float32"), "m1": ("psum", [128, 512], "float32"),
+           "m2": ("psum", [128, 512], "float32")}
 for _t, _b in (("int32", "pi 1 pm 1 w0 2 ec 16 eq 16"),
                ("uint16", "w16 16 w2 32 jj 4 oo 16 ou 4 oy 16"),
-               ("float32", "acc 1 e1 16 e2 16 e3 16 e4 16 b1 4 b2 4 b3 4 ys 256 yo 256"),
-               ("bfloat16", "k0 2 hf 2 s0 1 s1 1 gsc 1 vwin 2064 pos %d row 256 rt 256 cm 32 td 768 qf 272 "
-                            "ge 256 gh 256 cc 256 le 256 nn 256 sg 256 lg 64 lt 64 li 16 rl 4 xt 1024 xs %d "
-                            "wb 512 ta 512 tb 512 vp 64 pr 512 pt 512 p2 16 p3 16" % (8 * PO, 4 * XW)),
-               ("float8_e4m3fn_x4", "qw 128 qa 128 ca 128 cb 224 rc 128"),
-               ("uint8", "pw 128 pa 128 da 128 db 224 rs 128")):
+               ("float32", "acc 2 e1 16 e2 16 e3 16 e4 16 b1 4 b2 4 b3 4 ys 256 yo 256"),
+               ("bfloat16", "k0 2 hf 2 s0 1 g0 1 g1 1 vwin 2064 pos %d row 256 rt 256 pp 32 cm 32 td 768 qf 272 "
+                            "ge 768 cc 512 sg 512 lg 64 lt 64 li 16 rl 4 xt 1024 xs %d "
+                            "wb 512 tt 1152 vp 64 pr 512 pt 512 p2 16 p3 16" % (8 * PO, 4 * XW)),
+               ("float8_e4m3fn_x4", "qw 128 qa 128 qb 128 cb 352 rc 128"),
+               ("uint8", "pw 128 pa 128 pb 128 db 352 rs 128")):
     _w = _b.split()
     for _i in range(0, len(_w), 2):
         SCRATCH[_w[_i]] = ("sbuf", [128, int(_w[_i + 1])], _t)
-SEMAPHORES = "ld ldx ldw ld0 v s ps te la lb ac ad st su loc rl rp th tz tc hs oy j0 j1 j2 j3 j4 j5 j6 j7 j8 j9".split()
+SEMAPHORES = "ld ldx ldw ld0 v s ps te la lb lc aa ab ac st loc rl rp th tz tc tn hs oy j0 j1 j2 j3 j4 j5".split()
 QUARTERS = [slice(32 * a, 32 * a + 32) for a in range(4)]
 LOW, HIGH = slice(0, 64), slice(64, 128)
 
@@ -41,17 +42,13 @@ def roads(topo, cores, r):
     a = mine.index(r)
     f = [far[(h - a) % 4] for h in range(4)]
     m = [mine[(a + j) % 4] for j in range(4)]
-    return [same[0], other[0], same[1], other[1]], f + m[1:] + [r]
+    return [same[0], other[0], same[1], other[1]], f + [m[2], m[1], m[3], r]
 
 
-PLACES = 2
-JOBS = ((0, 0, (4, 5)), (1, 0, (6,)), (3, 1, (4, 5)), (1, 1, (6,)),
-        (0, 0, (0, 1)), (1, 0, (2, 3)), (2, 1, (0, 1)), (3, 1, (2, 3)))
-CALLS = ((0,), (1,), (2,), (3,), (4, 5), (6, 7))
-
-
-def width(i):
-    return 4 if any(i in c and len(c) == 4 for c in CALLS) else 8
+ORDER = (0, 1, 5, 6, None, 7, 2, 3, 4)
+ARRIVED = (7, 5, 6, 0, 1, 4, 2, 3)
+PLACES = 3
+JOBS = ((3, 0, (5, 6)), (1, 1, (5, 6)), (1, 0, (0, 1)), (3, 1, (0, 1)), (0, 0, (2, 3)), (2, 1, (2, 3)))
 
 
 def mask(engines):
@@ -69,21 +66,14 @@ def u8(view):
 
 
 def landing(T, run):
-    if run < 4:
-        at = slice(32 * run, 32 * run + 32)
-        return T.ca[:, at], T.da[:, at], T.sem.ac
-    at = slice(32 * run, 32 * run + 32)
-    return T.cb[:, at], T.db[:, at], T.sem.ad
+    a = 96 + 32 * ARRIVED.index(run)
+    return T.cb[:, a:a + 32], T.db[:, a:a + 32], T.sem.aa if run in (0, 1, 4) else T.sem.ab if run < 5 else T.sem.ac
 
 
 def stop(T, i, j=None):
     part, runs = JOBS[i][1:]
-    a = 64 * (runs[0] // 4)
-    return (T.rc, T.rs)[part][:, a:a + 32 * len(runs)] if j is None else (T.rc, T.rs)[part][:, a + 32 * j:a + 32 * j + 32]
-
-
-def column(run):
-    return 32 * run if run < 4 else 128 + 32 * ((run - 3) % 4 if run < 7 else 0)
+    a = 64 * (runs[0] // 2 % 2)
+    return (T.rc, T.rs)[part][:, a:a + 64] if j is None else (T.rc, T.rs)[part][:, a + 32 * j:a + 32 * j + 32]
 
 
 def relay(g, core, T, topo, r, h):
@@ -108,28 +98,25 @@ def relay(g, core, T, topo, r, h):
         left[0] += len(en)
     if h == PLACES:
         v(V.memset(T.k0[:, :], 0.5))
-    else:
+    elif h == 0:
         g.iota(T.pi[:, 0:1], [[0, 1]], 0, 1).then_inc(S.ps, 1)
         V.wait_ge(S.ps, 1)
-        if h < 2:
-            v(V.tensor_scalar(T.pm[:, :], T.pi[:, :], 15, None, OP.bitwise_and))
-            vw()
-            v(V.tensor_scalar(T.k0[:, 0:1], T.pm[:, :], 16.5 * h, None, OP.add))
-        else:
-            v(V.tensor_scalar(T.pm[:, :], T.pi[:, :], 4, 1, OP.arith_shift_right, OP.bitwise_and))
-            vw()
-            for a, q in enumerate(QUARTERS):
-                v(V.tensor_scalar(T.k0[q, 0:1], T.pm[q, :], -0.75 * 16.0 ** -a, 16.0 ** -a, OP.mult, OP.add))
+        v(V.tensor_scalar(T.pm[:, :], T.pi[:, :], 31, None, OP.bitwise_and))
+        vw()
+        v(V.tensor_scalar(T.k0[:, 0:1], T.pm[:, :], 0.5, None, OP.add))
+    else:
+        for a, q in enumerate(QUARTERS):
+            v(V.memset(T.k0[q, 0:1], 4.0 ** -(2 * a + (f if h == 2 else r) % 2)))
     g.wait_ge(S.v, n[0])
-    where = (T.s0[:, 0:1], T.s1[:, 0:1], T.hf[:, 0:2], T.gsc[:, 0:1])[h]
-    send(r, (S.th, S.th, S.tz, S.tc)[h], T.k0[:, 0:2 if h == PLACES else 1], where)
+    where = (T.s0[:, 0:1], T.g1[:, 0:1], T.g0[:, 0:1], T.hf[:, 0:2])[h]
+    send(r, (S.th, S.tn, S.tc, S.tz)[h], T.k0[:, 0:2 if h == PLACES else 1], where)
     if h == PLACES:
         D.wait_ge(S.hs, 16)
         for i in range(4):
             D.dma_start(T.wt[16 * i:16 * i + 16, :], T.hw[:, :]).then_inc(S.ld, 16)
         g.iota(T.pi[:, 0:1], [[0, 1]], 0, 1).then_inc(S.ps, 1)
         g.wait_ge(S.ps, 1)
-        col = [column(roads(topo, cores, q)[1].index(r)) for q in range(8)]
+        col = [32 * ARRIVED.index(roads(topo, cores, q)[1].index(r)) for q in range(8)]
         for a, q in enumerate(QUARTERS):
             g.iota(T.b1[q, :], [[PO, 2], [0, 2]], 2 * a * PO + 32, 0, **SMALL).then_inc(S.ps, 1)
             g.iota(T.b3[q, :], [[PO, 2], [16, 2]], 2 * a * PO, 0, **SMALL).then_inc(S.ps, 1)
@@ -138,7 +125,7 @@ def relay(g, core, T, topo, r, h):
         V.wait_ge(S.ps, 13)
         v(V.tensor_scalar(T.pm[:, :], T.pi[:, :], 15, None, OP.bitwise_and))
         vw()
-        v(V.tensor_copy(T.acc[:, :], T.pm[:, :]))
+        v(V.tensor_copy(T.acc[:, 0:1], T.pm[:, :]))
         vw()
         v(V.tensor_scalar(T.b2[:, :], T.b3[:, :], T.acc[:, 0:1], None, OP.add))
         V.wait_ge(S.ld, 64)
@@ -155,8 +142,7 @@ def relay(g, core, T, topo, r, h):
         for half in (LOW, HIGH):
             for k in range(2):
                 v(V.tensor_copy(T.w2[half, k:32:2], T.e4[LOW, :]))
-        V.wait_ge(S.rl, 8)
-        V.wait_ge(S.rp, 8)
+        V.wait_ge(S.rp, 16)
         vw()
         for k in range(4):
             v(V.tensor_scalar(T.ou[:, k:k + 1], T.rl[:, k:k + 1], T.b1[:, k:k + 1], T.b2[:, k:k + 1], OP.add, OP.max))
@@ -180,23 +166,21 @@ def relay(g, core, T, topo, r, h):
 
     if h % 2 == 0:
         g.wait_ge(S.rl, 8)
-        at = [2 * roads(topo, cores, k)[1].index(r) for k in slots[h:h + 2]]
-        g.remote_dma_fused([xfer(topo, core, cores[k], en[4 * i:4 * i + 4], S.la, T.rl[:, 2 * (f % 2):2 * (f % 2) + 2],
-                                 T.li[:, at[i]:at[i] + 2]) for i, k in enumerate(slots[h:h + 2])], local_sem=S.loc)
-        left[0] += len(en)
-    if h == PLACES:
-        g.wait_ge(S.rp, 8)
-        g.wait_ge(S.v, n[0])
-        send(r, S.oy, T.oy[:, 0:16], T.oy[:, 0:16])
+        for k in slots[h // 2:4:2]:
+            run = roads(topo, cores, k)[1].index(r)
+            send(k, (S.la, S.lc)[run // 2], T.rl[:, 2 * (f % 2):2 * (f % 2) + 2], T.li[:, 2 * run:2 * run + 2])
     for i, (k, part, runs) in enumerate(JOBS):
         if k == h:
             view = (u8, lambda a: a)[part]
             share = len(en) // len(runs)
-            g.wait_ge(S["j%d" % i], width(i))
+            g.wait_ge(S["j%d" % i], 16)
             g.remote_dma_fused([xfer(topo, core, cores[slots[run]], en[share * j:share * j + share], landing(T, run)[2],
                                      view(stop(T, i, j)), view(landing(T, run)[part]))
                                 for j, run in enumerate(runs)], local_sem=S.loc)
             left[0] += len(en)
+    if h == PLACES:
+        g.wait_ge(S.v, n[0])
+        send(r, S.oy, T.oy[:, 0:16], T.oy[:, 0:16])
     g.wait_ge(S.loc, left[0])
 
 
@@ -243,19 +227,13 @@ def rank_program(g, core, T, topo):
 
     D.dma_start(T.wt[0:16, :], T.want[:, :]).then_inc(S.ld, 16)
     A.dma_start(T.wt[16:32, :], T.want[:, :]).then_inc(S.ld, 16)
-    D.dma_start(T.wt[32:48, :], T.want[:, :]).then_inc(S.ld, 16)
-    A.dma_start(T.wt[48:64, :], T.want[:, :]).then_inc(S.ld, 16)
-    D.dma_start(T.w0[:, :], T.want[:, :]).then_inc(S.ld0, 16)
+    A.dma_start(T.w0[:, :], T.want[:, :]).then_inc(S.ld0, 16)
     D.dma_start(T.xt[:, :], T.x[:, :]).then_inc(S.ldx, 16)
     D.dma_start(T.wb[:, :], T.w[:, :]).then_inc(S.ldw, 16)
 
     none = 2048
-    g_v = ps(g.iota(T.vwin[:, 0:128], [[1, 128]], 128, 0, **SMALL))
-    v_z = v(V.memset(T.cm[LOW, :], -1.0))
-    g.wait_ge(S.v, v_z)
-    g.wait_ge(S.ps, g_v)
-    for q in QUARTERS[0:2]:
-        g_t = ps(g.affine_select(T.cm[q, :], T.cm[q, :], [[-1, 32]], OP.not_equal, 0.0, 0, 1))
+    made = [ps(g.iota(T.vwin[:, 128 * e:128 * e + 128], [[2 ** e, 128]], 128 * 2 ** e, 0, **SMALL)) for e in range(3)]
+    g_v, g_w = made[0], made[2]
     g.wait_ge(S.ld0, 16)
     send([(relays[PLACES], on, S.hs, T.w0[:, 0:2], T.hw[:, :])])
 
@@ -263,41 +241,44 @@ def rank_program(g, core, T, topo):
     v(V.memset(T.qf[:, 256:272], 0.0))
     v(V.memset(T.w16[HIGH, 14:16], none))
     v(V.memset(T.ne[:, :, 256:288], 1.0))
+    v(V.memset(T.td[:, 0:384], 0.0))
     V.wait_ge(S.ps, g_v)
     A.wait_ge(S.ps, g_v)
-    for e in range(1, 16):
+    for e in range(3, 16):
         if e <= 10:
             v(V.tensor_scalar(T.vwin[:, 128 * e:128 * e + 128], T.vwin[:, 0:128], 2.0 ** e, None, OP.mult))
         else:
             s_v = s(A.activation(T.vwin[:, 128 * e:128 * e + 128], T.vwin[:, 0:128], COPY, scale=2.0 ** e))
 
-    V.wait_ge(S.ld, 64)
-    v(V.tensor_copy(T.w16[LOW, :], T.wt[:, :]))
-    v_w = v(V.tensor_copy(T.w16[HIGH, 0:14], T.wt[:, 2:16]))
-    v(V.memset(T.td[:, 0:384], 0.0))
+    V.wait_ge(S.ld, 32)
+    for a, q in enumerate(QUARTERS):
+        v_w = v(V.tensor_copy(T.w16[q, 0:16 - 2 * (a // 2)], T.wt[0:32, 2 * (a // 2):16]))
+    v_p = v(V.transpose(T.pp[:, :], T.vwin[:, 0:32]))
     V.wait_ge(S.s, s_v)
+    V.wait_ge(S.ps, g_w)
+    A.wait_ge(S.ps, g_w)
     V.wait_ge(S.v, v_w)
     v_r = v(V.tensor_copy(T.row[:, 0:128], T.vwin[:, 0:none + 16].indirect(T.w16[:, 0:8])))
     v(V.memset(T.td[:, 384:768], 0.0))
     A.wait_ge(S.v, v_w)
     A.wait_ge(S.s, s_v)
     s_r = s(A.activation(T.row[:, 128:256], T.vwin[:, 0:none + 16].indirect(T.w16[:, 8:16]), COPY))
-    A.wait_ge(S.ps, g_t)
-    s_m = s(A.activation(T.cm[HIGH, :], T.cm[LOW, :], COPY))
+    A.wait_ge(S.v, v_p)
+    s_m = s(A.activation(T.cm[:, :], T.vwin[:, 0:32], ACT.Abs, bias=T.pp[:, 0:1], scale=-1.0))
     V.wait_ge(S.v, v_r)
     v_t0 = v(V.transpose(T.rt[:, 0:128], T.row[:, 0:128]))
     V.wait_ge(S.s, s_r)
     v_t1 = v(V.transpose(T.rt[:, 128:256], T.row[:, 128:256]))
     A.wait_ge(S.s, s_m)
     at = [0, 288, 512, 672]
-    ne, td = [], []
-    for b, turned in enumerate((v_t0, v_t0, v_t1, v_t1)):
+    ne, td = {}, {}
+    for b, turned in ((1, v_t0), (0, v_t0), (2, v_t1), (3, v_t1)):
         entry = T.rt[:, 64 * b:64 * b + 1]
         V.wait_ge(S.v, turned)
-        ne.append(v(V.tensor_scalar(T.ne[:, b, 64 * b:256], T.row[:, 64 * b:256], entry, None, OP.not_equal)))
+        ne[b] = v(V.tensor_scalar(T.ne[:, b, 64 * b:256], T.row[:, 64 * b:256], entry, None, OP.not_equal))
         A.wait_ge(S.v, turned)
-        td.append(s(A.activation(T.td[:, at[b]:at[b] + 32], T.cm[:, :], ACT.Relu, bias=entry, scale=2.0 ** 30)))
-    for b in range(4):
+        td[b] = s(A.activation(T.td[:, at[b]:at[b] + 32], T.cm[:, :], ACT.Relu, bias=entry, scale=-2.0 ** 30))
+    for b in ne:
         V.wait_ge(S.v, ne[b])
         V.wait_ge(S.s, td[b])
         v(V.tensor_tensor_scan(T.sc[:, b, 64 * b:287], T.ne[:, b, 64 * b:287], T.td[:, at[b]:at[b] + 287 - 64 * b],
@@ -309,122 +290,137 @@ def rank_program(g, core, T, topo):
 
     A.wait_ge(S.ldx, 16)
     for t in range(4):
-        s_xs = s(A.activation(T.xs[:, XW * t:XW * t + 128], T.xt[:, t:512:4], COPY))
+        s(A.activation(T.xs[:, XW * t:XW * t + 128], T.xt[:, t:512:4], COPY))
 
-    def upper(t):
-        for k in range(2):
-            v(V.tensor_copy(T.xs[:, XW * t + 128 + k:XW * t + XW:2], T.xt[:, 512 + t:1024:4]))
+    scale = (T.g0[:, 0:1], T.g1[:, 0:1])
 
+    low = (1 - r % 2, r % 2)
+
+    def beyond(k, a, b):
+        return v(V.tensor_scalar(T.ge[:, 256 * k + a:256 * k + b], T.qf[:, a:b], scale[0], 128.0 * 4.0 ** (k - low[0]),
+                                 OP.mult, OP.is_ge))
+
+    def counts(i, after):
+        part, k = slice(256 * i, 256 * i + 256), 256 * low[i]
+        V.wait_ge(S.v, after)
+        A.wait_ge(S.v, v(V.tensor_tensor_scan(T.cc[:, part], T.ge[:, k:k + 256], T.ge[:, k + 256:k + 512], 0.0,
+                                              OP.add, OP.subtract)))
+        return s(A.activation(T.sg[:, part], T.cc[:, part], ACT.Sign, bias=T.s0[:, 0:1], scale=-1.0,
+                              accum_out=T.acc[:, i:i + 1]))
+
+    def entries(i, after):
+        V.wait_ge(S.s, after)
+        return v(V.tensor_scalar(T.jj[:, 2 * i:2 * i + 2], T.hf[:, :], T.acc[:, i:i + 1], 128.0, OP.mult, OP.add))
+
+    def columns(i, after):
+        V.wait_ge(S.v, after)
+        return v(V.tensor_scalar(T.lg[:, 32 * i:32 * i + 32], T.qf[:, 0:272].indirect(T.jj[:, 2 * i:2 * i + 2]),
+                                 scale[i], -128.0, OP.mult, OP.add))
+
+    def turn(i, after):
+        V.wait_ge(S.v, after)
+        return v(V.transpose(T.lt[:, 32 * i:32 * i + 32], T.lg[:, 32 * i:32 * i + 32]))
     V.wait_ge(S.tc, 8)
-    parts = (slice(0, 128), slice(128, 256))
-    for k, part in enumerate(parts):
-        V.wait_ge(S.v, turned[k])
-        v(V.tensor_scalar(T.ge[:, part], T.qf[:, part], T.gsc[:, 0:1], 128.0, OP.mult, OP.is_ge))
-        v(V.tensor_scalar(T.gh[:, part], T.qf[:, part], T.gsc[:, 0:1], 512.0, OP.mult, OP.is_ge))
-    vw()
-    v_c = v(V.tensor_tensor_scan(T.cc[:, :], T.ge[:, :], T.gh[:, :], 0.0, OP.add, OP.subtract))
-    V.wait_ge(S.ldx, 16)
-    upper(0)
-    V.wait_ge(S.th, 16)
-    V.wait_ge(S.v, v_c)
-    le = [v(V.tensor_scalar(T.le[:, part], T.cc[:, part], T.s0[:, 0:1], None, OP.is_le)) for part in parts]
-    for k, part in enumerate(parts):
-        V.wait_ge(S.v, le[k])
-        v(V.tensor_tensor_scan(T.nn[:, part], T.le[:, part], T.td[:, 32:160], 0.0, OP.add, OP.add))
-    A.wait_ge(S.th, 16)
-    A.wait_ge(S.v, v_c)
-    s_n = s(A.activation(T.sg[:, :], T.cc[:, :], ACT.Sign, bias=T.s1[:, 0:1], scale=-1.0, accum_out=T.acc[:, 0:1]))
-    V.wait_ge(S.tz, 8)
-    V.wait_ge(S.s, s_n)
-    v(V.tensor_scalar(T.jj[:, 2:4], T.hf[:, :], T.acc[:, 0:1], 128.0, OP.mult, OP.add))
-    V.wait_ge(S.v, n["v"] - 1)
-    v(V.tensor_scalar(T.jj[:, 0:2], T.td[:, 32:34], T.nn[:, 127:128], T.nn[:, 255:256], OP.add, OP.add))
-    upper(1)
-    V.wait_ge(S.v, n["v"] - 2)
-    v(V.tensor_scalar(T.lg[:, :], T.qf[:, 0:272].indirect(T.jj[:, 0:4]), T.gsc[:, 0:1], -128.0, OP.mult, OP.add))
-    upper(2)
-    V.wait_ge(S.v, n["v"] - 2)
     for k in range(2):
-        v_msg = v(V.transpose(T.lt[:, k:64:2], T.lg[:, 32 * k:32 * k + 32]))
-    upper(3)
+        V.wait_ge(S.v, turned[k])
+        v_f = [beyond(low[0] + j, 128 * k, 128 * k + 128) for j in range(2)][-1]
+    v_n = beyond(2 * low[1], 0, 256)
+    A.wait_ge(S.th, 8)
+    s_f = counts(0, v_f)
+    s_n = counts(1, v_n)
+    for t in range(4):
+        s_xs = s(A.activation(T.xs[:, XW * t + 128:XW * t + XW:2], T.xt[:, 512 + t:1024:4], COPY))
+    V.wait_ge(S.tz, 8)
+    V.wait_ge(S.tn, 8)
+    v_f, v_n = entries(0, s_f), entries(1, s_n)
+    v_f, v_n = columns(0, v_f), columns(1, v_n)
+    v_f, v_msg = turn(0, v_f), turn(1, v_n)
+    V.wait_ge(S.ldw, 16)
+    v(V.quantize_mx(T.qw[:, :], T.pw[:, :], T.wb[:, :]))
 
-    def of(f):
-        return T.lt[:, 30 + 2 * (f % 2):32 + 2 * (f % 2)]
+    theirs, ours = T.lt[:, 15:17], T.lt[:, 47:49]
 
     def to(f, engines):
-        k = 2 * roads(topo, cores, f)[1].index(r)
-        return cores[f], engines, S.lb, of(f), T.li[:, k:k + 2]
+        run = roads(topo, cores, f)[1].index(r)
+        return cores[f], engines, S.lc if run == 4 else S.lb, ours, T.li[:, 2 * run:2 * run + 2]
     far, near = 2 * (slots[0] % 2), 2 * (r % 2)
+    g.wait_ge(S.v, v_f)
+    send([(c, on[8 * i:8 * i + 8], S.rl, theirs, T.rl[:, far:far + 2]) for i, c in enumerate(relays[0::2])])
     g.wait_ge(S.v, v_msg)
-    send([(c, on[8 * i:8 * i + 8], S.rl, of(slots[0]), T.rl[:, far:far + 2]) for i, c in enumerate(relays[0::2])])
-    send([to(slots[4], off[0:4]), to(slots[5], off[4:8]), (relays[PLACES], on[0:8], S.rp, of(r), T.rl[:, near:near + 2])])
-    send([to(slots[6], off)])
+    send([to(slots[5], off[0:4]), to(slots[6], off[4:8])])
+    send([to(slots[4], off)])
+    send([(relays[PLACES], on[0:8], S.rp, theirs, T.rl[:, far:far + 2]), (relays[PLACES], off, S.rp, ours, T.rl[:, near:near + 2])])
 
     mq = QUARTERS[r // 2]
 
     def spread(a, b, lists):
         return [v(V.tensor_copy(T.oo[q, 2 * a:2 * b], lists)) for q in QUARTERS][-1]
 
-    def gather(a, b, ready):
-        tile = (T.ta, T.tb)[a // 4]
-        sides = [(tile[:, 128 * (a % 4) + t:128 * ((b - 1) % 4 + 1):4],
-                  T.xs[:, XW * t:XW * t + XW].indirect(T.oo[:, 2 * a:2 * b])) for t in range(4)]
+    def side(a, b, t):
+        at = 128 * ORDER.index(a)
+        return T.tt[:, at + t:at + 128 * (b - a):4], T.xs[:, XW * t:XW * t + XW].indirect(T.oo[:, 2 * a:2 * b])
+
+    def gather(a, b, k=2):
+        return ([v(V.tensor_copy(*side(a, b, t))) for t in range(k)][-1],
+                [s(A.activation(*side(a, b, t), COPY)) for t in range(k, 4)][-1])
+
+    def both(ready):
         V.wait_ge(S.v, ready)
         A.wait_ge(S.v, ready)
-        return [v(V.tensor_copy(*x)) for x in sides[0:2]][-1], [s(A.activation(*x, COPY)) for x in sides[2:4]][-1]
 
-    def pack(codes, scales, tile, made):
+    def pack(codes, scales, at, made):
         V.wait_ge(S.v, made[0])
         V.wait_ge(S.s, made[1])
-        return v(V.quantize_mx(codes[:, 0:128], scales[:, 0:128], tile[:, :]))
+        return v(V.quantize_mx(codes[:, 0:128], scales[:, 0:128], T.tt[:, 128 * at:128 * at + 512]))
+    v(V.memset(T.tt[:, 128 * ORDER.index(None):128 * ORDER.index(None) + 128], 0.0))
     V.wait_ge(S.v, v_msg)
-    v_o = spread(7, 8, T.lt[mq, 30 + near:32 + near])
-    V.wait_ge(S.ldw, 16)
-    v_qw = v(V.quantize_mx(T.qw[:, :], T.pw[:, :], T.wb[:, :]))
+    v_o = spread(7, 8, T.lt[mq, 47:49])
     V.wait_ge(S.s, s_xs)
     A.wait_ge(S.s, s_xs)
-    gather(7, 8, v_o)
-    V.wait_ge(S.lb, 16)
-    made = gather(4, 7, spread(4, 7, T.li[mq, 8:14]))
+    both(v_o)
+    gather(7, 8)
+    V.wait_ge(S.lb, 8)
+    both(spread(5, 7, T.li[mq, 10:14]))
+    made = gather(5, 7)
     V.wait_ge(S.la, 16)
-    v_o = spread(0, 4, T.li[mq, 0:8])
-    v_near = pack(T.cb, T.db, T.tb, made)
-    v_far = pack(T.qa, T.pa, T.ta, gather(0, 4, v_o))
+    first = spread(0, 2, T.li[mq, 0:4])
+    packed = [pack(T.cb, T.db, 2, made)]
+    V.wait_ge(S.lc, 24)
+    second = spread(2, 5, T.li[mq, 4:10])
+    both(first)
+    made = [gather(0, 2)]
+    both(second)
+    made.append(gather(2, 5))
+    packed += [pack(T.qa, T.pa, 0, made[0]), pack(T.qb, T.pb, 5, made[1])]
 
-    g.wait_ge(S.v, v_near)
-
-    def job(i):
-        h, part, runs = JOBS[i]
-        src = ((T.qa, T.cb), (T.pa, T.db))[part][runs[0] // 4][:, 32 * (runs[0] % 4):32 * (runs[-1] % 4 + 1)]
+    for i, (h, part, runs) in enumerate(JOBS):
+        if part == 0:
+            g.wait_ge(S.v, packed[i // 2])
+        a = 32 * (i // 4)
+        src = ((T.cb, T.qa, T.qb), (T.db, T.pa, T.pb))[part][i // 2][:, a:a + 64]
         view = (u8, lambda a: a)[part]
-        k = width(i) * (i % (16 // width(i)))
-        return relays[h], on[k:k + width(i)], S["j%d" % i], view(src), view(stop(T, i))
-    for call in CALLS:
-        if JOBS[call[0]][2][0] < 4:
-            g.wait_ge(S.v, v_far)
-        send([job(i) for i in call])
+        send([(relays[h], on, S["j%d" % i], view(src), view(stop(T, i)))])
+    send([(cores[slots[4]], off, S.aa, u8(T.qb[:, 96:128]), u8(landing(T, 4)[0]))])
+    send([(cores[slots[4]], off, S.aa, T.pb[:, 96:128], landing(T, 4)[1])])
     g.wait_ge(S.loc, n["loc"])
 
-    P.wait_ge(S.v, v_near)
-    P.wait_ge(S.ad, 32)
-    P.matmul_mx(T.m1[:, 0:128], T.qw[:, :], T.pw[:, :], T.cb[:, 96:224], T.db[:, 96:224], True, True).then_inc(S.te, 1)
-    P.wait_ge(S.ac, 8 * sum(runs[0] < 4 for _, _, runs in JOBS))
-    P.matmul_mx(T.m0[:, 0:128], T.qw[:, :], T.pw[:, :], T.ca[:, :], T.da[:, :], True, True).then_inc(S.te, 1)
+    P.wait_ge(S.v, packed[0])
+    for out, a, sem, writes in ((T.m0, 64, S.ac, 2), (T.m1, 160, S.aa, 4), (T.m2, 224, S.ab, 2)):
+        P.wait_ge(sem, 8 * writes)
+        P.matmul_mx(out[:, 0:128], T.qw[:, :], T.pw[:, :], T.cb[:, a:a + 128], T.db[:, a:a + 128], True, True).then_inc(S.te, 1)
     A.wait_ge(S.te, 1)
-    s_y = s(A.activation(T.ys[:, 128:256], T.m1[:, 0:128], COPY))
+    s(A.activation(T.ys[:, 0:96], T.m0[:, 32:128], COPY))
+    A.wait_ge(S.te, 2)
+    s_y = s(A.activation(T.ys[:, 96:192], T.m1[:, 32:128], COPY))
     V.wait_ge(S.oy, 8)
     A.wait_ge(S.oy, 8)
-    V.wait_ge(S.te, 2)
-    v_y = v(V.tensor_copy(T.ys[:, 0:128], T.m0[:, 0:128]))
+    V.wait_ge(S.te, 3)
+    v_y = v(V.tensor_copy(T.ys[:, 192:256], T.m2[:, 64:128]))
     vw()
     V.wait_ge(S.s, s_y)
-    v_o = v(V.tensor_copy(T.yo[:, 0:128], T.ys[:, 0:256].indirect(T.oy[:, 0:8])))
+    D.wait_ge(S.v, v(V.tensor_copy(T.yo[:, 0:128], T.ys[:, :].indirect(T.oy[:, 0:8]))))
     A.wait_ge(S.v, v_y)
     A.wait_ge(S.s, s_y)
-    s_o = s(A.activation(T.yo[:, 128:256], T.ys[:, 0:256].indirect(T.oy[:, 8:16]), COPY))
-    D.wait_ge(S.v, v_o)
-    D.dma_start(T.y[:, 0:128], T.yo[:, 0:128]).then_inc(S.st, 16)
-    A.wait_ge(S.s, s_o)
-    A.dma_start(T.y[:, 128:256], T.yo[:, 128:256]).then_inc(S.su, 16)
+    D.wait_ge(S.s, s(A.activation(T.yo[:, 128:256], T.ys[:, :].indirect(T.oy[:, 8:16]), COPY)))
+    D.dma_start(T.y[:, :], T.yo[:, :]).then_inc(S.st, 16)
     D.wait_ge(S.st, 16)
-    A.wait_ge(S.su, 16)

from concourse.bass import DstId, RemoteDMATransfer
from concourse.mybir import dt, AluOpType, ActivationFunctionType

OP = AluOpType
ACT = ActivationFunctionType
COPY = ACT.Copy
XW = 384
PO = 32 + XW
SMALL = {"allow_small_or_imprecise_dtypes": True}

SCRATCH = {"wt": ("sbuf", [64, 16], "int32"), "hw": ("dram", [128, 2], "int32"),
           "ne": ("sbuf", [128, 4, 288], "bfloat16"), "sc": ("sbuf", [128, 4, 288], "bfloat16"),
           "m0": ("psum", [128, 512], "float32"), "m1": ("psum", [128, 512], "float32"),
           "m2": ("psum", [128, 512], "float32")}
for _t, _b in (("int32", "pi 1 pm 1 w0 2 ec 16 eq 16"),
               ("uint16", "w16 16 w2 32 jj 4 oo 16 ou 4 oy 16"),
               ("float32", "acc 2 e1 16 e2 16 e3 16 e4 16 b1 4 b2 4 b3 4 ys 256 yo 256"),
               ("bfloat16", "k0 2 hf 2 s0 1 g0 1 g1 1 vwin 2064 pos %d row 256 rt 256 pp 32 cm 32 td 768 qf 272 "
                            "ge 768 cc 512 sg 512 lg 64 lt 64 li 16 rl 4 xt 1024 xs %d "
                            "wb 512 tt 1152 vp 64 pr 512 pt 512 p2 16 p3 16" % (8 * PO, 4 * XW)),
               ("float8_e4m3fn_x4", "qw 128 qa 128 qb 128 cb 352 rc 128"),
               ("uint8", "pw 128 pa 128 pb 128 db 352 rs 128")):
    _w = _b.split()
    for _i in range(0, len(_w), 2):
        SCRATCH[_w[_i]] = ("sbuf", [128, int(_w[_i + 1])], _t)
SEMAPHORES = "ld ldx ldw ld0 v s ps te la lb lc aa ab ac st loc rl rp th tz tc tn hs oy j0 j1 j2 j3 j4 j5".split()
QUARTERS = [slice(32 * a, 32 * a + 32) for a in range(4)]
LOW, HIGH = slice(0, 64), slice(64, 128)


def plane_of(topo, cores, r):
    return [k for k in range(len(cores)) if k == r or topo.same_plane(cores[k], cores[r])]


def roads(topo, cores, r):
    mine = plane_of(topo, cores, r)
    far = [k for k in range(len(cores)) if k not in mine]
    c = cores[r]
    able = [k for k in topo.cores_of(c) if k != c and all(topo.may_write(k, cores[f]) for f in far)]
    same = [k for k in able if topo.die(k) == topo.die(c)]
    other = [k for k in able if topo.die(k) != topo.die(c)]
    a = mine.index(r)
    f = [far[(h - a) % 4] for h in range(4)]
    m = [mine[(a + j) % 4] for j in range(4)]
    return [same[0], other[0], same[1], other[1]], f + [m[2], m[1], m[3], r]


ORDER = (0, 1, 5, 6, None, 7, 2, 3, 4)
ARRIVED = (7, 5, 6, 0, 1, 4, 2, 3)
PLACES = 3
JOBS = ((3, 0, (5, 6)), (1, 1, (5, 6)), (1, 0, (0, 1)), (3, 1, (0, 1)), (0, 0, (2, 3)), (2, 1, (2, 3)))


def mask(engines):
    return sum(1 << k for k in engines)


def xfer(topo, src_core, dst_core, engines, sem, src, dst):
    rid, pid = topo.addr(dst_core, src_core)
    return RemoteDMATransfer(dst_ids=[DstId(rid=rid, pnc=pid)], dma_engine_mask=mask(engines),
                             remote_sem=sem, srcs=[src], dsts=[dst], alu_op=0)


def u8(view):
    return view.bitcast(dt.uint8)


def landing(T, run):
    a = 96 + 32 * ARRIVED.index(run)
    return T.cb[:, a:a + 32], T.db[:, a:a + 32], T.sem.aa if run in (0, 1, 4) else T.sem.ab if run < 5 else T.sem.ac


def stop(T, i, j=None):
    part, runs = JOBS[i][1:]
    a = 64 * (runs[0] // 2 % 2)
    return (T.rc, T.rs)[part][:, a:a + 64] if j is None else (T.rc, T.rs)[part][:, a + 32 * j:a + 32 * j + 32]


def relay(g, core, T, topo, r, h):
    cores = T.cores
    slots = roads(topo, cores, r)[1]
    f = slots[h]
    en = topo.engines(core, cores[f])
    V, A, D, S = g.vector, g.scalar, g.sync, T.sem
    n = [0]
    left = [0]

    def v(call):
        call.then_inc(S.v, 1)
        n[0] += 1

    def vw():
        V.wait_ge(S.v, n[0])

    def send(k, sem, src, dst):
        rid, pid = topo.addr(cores[k], core)
        g.remote_dma(dst, src, sem, S.loc, pid, rid, mask(en))
        left[0] += len(en)
    if h == PLACES:
        v(V.memset(T.k0[:, :], 0.5))
    elif h == 0:
        g.iota(T.pi[:, 0:1], [[0, 1]], 0, 1).then_inc(S.ps, 1)
        V.wait_ge(S.ps, 1)
        v(V.tensor_scalar(T.pm[:, :], T.pi[:, :], 31, None, OP.bitwise_and))
        vw()
        v(V.tensor_scalar(T.k0[:, 0:1], T.pm[:, :], 0.5, None, OP.add))
    else:
        for a, q in enumerate(QUARTERS):
            v(V.memset(T.k0[q, 0:1], 4.0 ** -(2 * a + (f if h == 2 else r) % 2)))
    g.wait_ge(S.v, n[0])
    where = (T.s0[:, 0:1], T.g1[:, 0:1], T.g0[:, 0:1], T.hf[:, 0:2])[h]
    send(r, (S.th, S.tn, S.tc, S.tz)[h], T.k0[:, 0:2 if h == PLACES else 1], where)
    if h == PLACES:
        D.wait_ge(S.hs, 16)
        for i in range(4):
            D.dma_start(T.wt[16 * i:16 * i + 16, :], T.hw[:, :]).then_inc(S.ld, 16)
        g.iota(T.pi[:, 0:1], [[0, 1]], 0, 1).then_inc(S.ps, 1)
        g.wait_ge(S.ps, 1)
        col = [32 * ARRIVED.index(roads(topo, cores, q)[1].index(r)) for q in range(8)]
        for a, q in enumerate(QUARTERS):
            g.iota(T.b1[q, :], [[PO, 2], [0, 2]], 2 * a * PO + 32, 0, **SMALL).then_inc(S.ps, 1)
            g.iota(T.b3[q, :], [[PO, 2], [16, 2]], 2 * a * PO, 0, **SMALL).then_inc(S.ps, 1)
            g.iota(T.vp[q, :], [[col[2 * a + 1] - col[2 * a], 2], [1, 32]], col[2 * a], 0, **SMALL).then_inc(S.ps, 1)
        v(V.memset(T.pos[:, :], 0.0))
        V.wait_ge(S.ps, 13)
        v(V.tensor_scalar(T.pm[:, :], T.pi[:, :], 15, None, OP.bitwise_and))
        vw()
        v(V.tensor_copy(T.acc[:, 0:1], T.pm[:, :]))
        vw()
        v(V.tensor_scalar(T.b2[:, :], T.b3[:, :], T.acc[:, 0:1], None, OP.add))
        V.wait_ge(S.ld, 64)
        v(V.tensor_scalar(T.ec[LOW, :], T.wt[:, :], 255, None, OP.bitwise_and))
        v(V.tensor_scalar(T.eq[LOW, :], T.wt[:, :], 8, None, OP.arith_shift_right))
        vw()
        v(V.tensor_scalar(T.e1[LOW, :], T.ec[LOW, :], 2.0, -128.0, OP.mult, OP.add))
        v(V.tensor_scalar(T.e2[LOW, :], T.eq[LOW, :], float(PO), 32.0, OP.mult, OP.add))
        vw()
        v(V.tensor_tensor(T.e3[LOW, :], T.e1[LOW, :], T.ec[LOW, :], OP.max))
        vw()
        v(V.tensor_tensor(T.e4[LOW, :], T.e3[LOW, :], T.e2[LOW, :], OP.add))
        vw()
        for half in (LOW, HIGH):
            for k in range(2):
                v(V.tensor_copy(T.w2[half, k:32:2], T.e4[LOW, :]))
        V.wait_ge(S.rp, 16)
        vw()
        for k in range(4):
            v(V.tensor_scalar(T.ou[:, k:k + 1], T.rl[:, k:k + 1], T.b1[:, k:k + 1], T.b2[:, k:k + 1], OP.add, OP.max))
        vw()
        v(V.tensor_copy(T.pos[:, :].indirect(T.ou[:, 0:4]), T.vp[:, :]))
        A.wait_ge(S.v, n[0])
        A.activation(T.pr[:, 256:512], T.pos[:, :].indirect(T.w2[:, 16:32]), COPY).then_inc(S.s, 1)
        vw()
        v(V.tensor_copy(T.pr[:, 0:256], T.pos[:, :].indirect(T.w2[:, 0:16])))
        vw()
        v(V.transpose(T.pt[:, 0:256], T.pr[:, 0:256]))
        V.wait_ge(S.s, 1)
        v(V.transpose(T.pt[:, 256:512], T.pr[:, 256:512]))
        vw()
        v(V.tensor_tensor(T.p2[LOW, :], T.pt[LOW, 0:512:32], T.pt[HIGH, 0:512:32], OP.add))
        vw()
        v(V.tensor_tensor(T.p3[QUARTERS[0], :], T.p2[QUARTERS[0], :], T.p2[QUARTERS[1], :], OP.add))
        vw()
        for q in QUARTERS:
            v(V.tensor_copy(T.oy[q, :], T.p3[QUARTERS[0], :]))

    if h % 2 == 0:
        g.wait_ge(S.rl, 8)
        for k in slots[h // 2:4:2]:
            run = roads(topo, cores, k)[1].index(r)
            send(k, (S.la, S.lc)[run // 2], T.rl[:, 2 * (f % 2):2 * (f % 2) + 2], T.li[:, 2 * run:2 * run + 2])
    for i, (k, part, runs) in enumerate(JOBS):
        if k == h:
            view = (u8, lambda a: a)[part]
            share = len(en) // len(runs)
            g.wait_ge(S["j%d" % i], 16)
            g.remote_dma_fused([xfer(topo, core, cores[slots[run]], en[share * j:share * j + share], landing(T, run)[2],
                                     view(stop(T, i, j)), view(landing(T, run)[part]))
                                for j, run in enumerate(runs)], local_sem=S.loc)
            left[0] += len(en)
    if h == PLACES:
        g.wait_ge(S.v, n[0])
        send(r, S.oy, T.oy[:, 0:16], T.oy[:, 0:16])
    g.wait_ge(S.loc, left[0])


def rank_program(g, core, T, topo):
    cores = T.cores
    r = T.rank_of(core)
    if r is None:
        for k in range(len(cores)):
            if core in topo.cores_of(cores[k]):
                for h, c in enumerate(roads(topo, cores, k)[0]):
                    if c == core:
                        relay(g, core, T, topo, k, h)
        return
    S = T.sem
    relays, slots = roads(topo, cores, r)
    assert all((k in plane_of(topo, cores, r)) == (k % 2 == r % 2) for k in range(8))
    h_rid, h_pid = topo.addr(relays[PLACES], core)
    off = topo.engines(core, cores[slots[6]])
    on = topo.engines(core, relays[0])
    on = [e for e in on if e not in off] + off
    V, A, D, P = g.vector, g.scalar, g.sync, g.tensor
    n = {"v": 0, "s": 0, "ps": 0, "loc": 0}

    def count(name, call):
        call.then_inc(S[name], 1)
        n[name] += 1
        return n[name]

    def v(call):
        return count("v", call)

    def s(call):
        return count("s", call)

    def ps(call):
        return count("ps", call)

    def vw():
        V.wait_ge(S.v, n["v"])

    def send(transfers):
        g.remote_dma_fused([xfer(topo, core, *t) for t in transfers], local_sem=S.loc)
        n["loc"] += sum(len(t[1]) for t in transfers)

    D.dma_start(T.wt[0:16, :], T.want[:, :]).then_inc(S.ld, 16)
    A.dma_start(T.wt[16:32, :], T.want[:, :]).then_inc(S.ld, 16)
    A.dma_start(T.w0[:, :], T.want[:, :]).then_inc(S.ld0, 16)
    D.dma_start(T.xt[:, :], T.x[:, :]).then_inc(S.ldx, 16)
    D.dma_start(T.wb[:, :], T.w[:, :]).then_inc(S.ldw, 16)

    none = 2048
    made = [ps(g.iota(T.vwin[:, 128 * e:128 * e + 128], [[2 ** e, 128]], 128 * 2 ** e, 0, **SMALL)) for e in range(3)]
    g_v, g_w = made[0], made[2]
    g.wait_ge(S.ld0, 16)
    send([(relays[PLACES], on, S.hs, T.w0[:, 0:2], T.hw[:, :])])

    v(V.memset(T.vwin[:, none:none + 16], 0.0))
    v(V.memset(T.qf[:, 256:272], 0.0))
    v(V.memset(T.w16[HIGH, 14:16], none))
    v(V.memset(T.ne[:, :, 256:288], 1.0))
    v(V.memset(T.td[:, 0:384], 0.0))
    V.wait_ge(S.ps, g_v)
    A.wait_ge(S.ps, g_v)
    for e in range(3, 16):
        if e <= 10:
            v(V.tensor_scalar(T.vwin[:, 128 * e:128 * e + 128], T.vwin[:, 0:128], 2.0 ** e, None, OP.mult))
        else:
            s_v = s(A.activation(T.vwin[:, 128 * e:128 * e + 128], T.vwin[:, 0:128], COPY, scale=2.0 ** e))

    V.wait_ge(S.ld, 32)
    for a, q in enumerate(QUARTERS):
        v_w = v(V.tensor_copy(T.w16[q, 0:16 - 2 * (a // 2)], T.wt[0:32, 2 * (a // 2):16]))
    v_p = v(V.transpose(T.pp[:, :], T.vwin[:, 0:32]))
    V.wait_ge(S.s, s_v)
    V.wait_ge(S.ps, g_w)
    A.wait_ge(S.ps, g_w)
    V.wait_ge(S.v, v_w)
    v_r = v(V.tensor_copy(T.row[:, 0:128], T.vwin[:, 0:none + 16].indirect(T.w16[:, 0:8])))
    v(V.memset(T.td[:, 384:768], 0.0))
    A.wait_ge(S.v, v_w)
    A.wait_ge(S.s, s_v)
    s_r = s(A.activation(T.row[:, 128:256], T.vwin[:, 0:none + 16].indirect(T.w16[:, 8:16]), COPY))
    A.wait_ge(S.v, v_p)
    s_m = s(A.activation(T.cm[:, :], T.vwin[:, 0:32], ACT.Abs, bias=T.pp[:, 0:1], scale=-1.0))
    V.wait_ge(S.v, v_r)
    v_t0 = v(V.transpose(T.rt[:, 0:128], T.row[:, 0:128]))
    V.wait_ge(S.s, s_r)
    v_t1 = v(V.transpose(T.rt[:, 128:256], T.row[:, 128:256]))
    A.wait_ge(S.s, s_m)
    at = [0, 288, 512, 672]
    ne, td = {}, {}
    for b, turned in ((1, v_t0), (0, v_t0), (2, v_t1), (3, v_t1)):
        entry = T.rt[:, 64 * b:64 * b + 1]
        V.wait_ge(S.v, turned)
        ne[b] = v(V.tensor_scalar(T.ne[:, b, 64 * b:256], T.row[:, 64 * b:256], entry, None, OP.not_equal))
        A.wait_ge(S.v, turned)
        td[b] = s(A.activation(T.td[:, at[b]:at[b] + 32], T.cm[:, :], ACT.Relu, bias=entry, scale=-2.0 ** 30))
    for b in ne:
        V.wait_ge(S.v, ne[b])
        V.wait_ge(S.s, td[b])
        v(V.tensor_tensor_scan(T.sc[:, b, 64 * b:287], T.ne[:, b, 64 * b:287], T.td[:, at[b]:at[b] + 287 - 64 * b],
                               0.0, OP.mult, OP.add))
    vw()
    turned = [v(V.transpose(T.qf[:, 0:128], T.sc[:, :, 255:287]))]
    v(V.transpose(T.qf[HIGH, 128:256], T.sc[LOW, :, 255:287]))
    turned.append(v(V.transpose(T.qf[LOW, 128:256], T.sc[HIGH, :, 255:287])))

    A.wait_ge(S.ldx, 16)
    for t in range(4):
        s(A.activation(T.xs[:, XW * t:XW * t + 128], T.xt[:, t:512:4], COPY))

    scale = (T.g0[:, 0:1], T.g1[:, 0:1])

    low = (1 - r % 2, r % 2)

    def beyond(k, a, b):
        return v(V.tensor_scalar(T.ge[:, 256 * k + a:256 * k + b], T.qf[:, a:b], scale[0], 128.0 * 4.0 ** (k - low[0]),
                                 OP.mult, OP.is_ge))

    def counts(i, after):
        part, k = slice(256 * i, 256 * i + 256), 256 * low[i]
        V.wait_ge(S.v, after)
        A.wait_ge(S.v, v(V.tensor_tensor_scan(T.cc[:, part], T.ge[:, k:k + 256], T.ge[:, k + 256:k + 512], 0.0,
                                              OP.add, OP.subtract)))
        return s(A.activation(T.sg[:, part], T.cc[:, part], ACT.Sign, bias=T.s0[:, 0:1], scale=-1.0,
                              accum_out=T.acc[:, i:i + 1]))

    def entries(i, after):
        V.wait_ge(S.s, after)
        return v(V.tensor_scalar(T.jj[:, 2 * i:2 * i + 2], T.hf[:, :], T.acc[:, i:i + 1], 128.0, OP.mult, OP.add))

    def columns(i, after):
        V.wait_ge(S.v, after)
        return v(V.tensor_scalar(T.lg[:, 32 * i:32 * i + 32], T.qf[:, 0:272].indirect(T.jj[:, 2 * i:2 * i + 2]),
                                 scale[i], -128.0, OP.mult, OP.add))

    def turn(i, after):
        V.wait_ge(S.v, after)
        return v(V.transpose(T.lt[:, 32 * i:32 * i + 32], T.lg[:, 32 * i:32 * i + 32]))
    V.wait_ge(S.tc, 8)
    for k in range(2):
        V.wait_ge(S.v, turned[k])
        v_f = [beyond(low[0] + j, 128 * k, 128 * k + 128) for j in range(2)][-1]
    v_n = beyond(2 * low[1], 0, 256)
    A.wait_ge(S.th, 8)
    s_f = counts(0, v_f)
    s_n = counts(1, v_n)
    for t in range(4):
        s_xs = s(A.activation(T.xs[:, XW * t + 128:XW * t + XW:2], T.xt[:, 512 + t:1024:4], COPY))
    V.wait_ge(S.tz, 8)
    V.wait_ge(S.tn, 8)
    v_f, v_n = entries(0, s_f), entries(1, s_n)
    v_f, v_n = columns(0, v_f), columns(1, v_n)
    v_f, v_msg = turn(0, v_f), turn(1, v_n)
    V.wait_ge(S.ldw, 16)
    v(V.quantize_mx(T.qw[:, :], T.pw[:, :], T.wb[:, :]))

    theirs, ours = T.lt[:, 15:17], T.lt[:, 47:49]

    def to(f, engines):
        run = roads(topo, cores, f)[1].index(r)
        return cores[f], engines, S.lc if run == 4 else S.lb, ours, T.li[:, 2 * run:2 * run + 2]
    far, near = 2 * (slots[0] % 2), 2 * (r % 2)
    g.wait_ge(S.v, v_f)
    send([(c, on[8 * i:8 * i + 8], S.rl, theirs, T.rl[:, far:far + 2]) for i, c in enumerate(relays[0::2])])
    g.wait_ge(S.v, v_msg)
    send([to(slots[5], off[0:4]), to(slots[6], off[4:8])])
    send([to(slots[4], off)])
    send([(relays[PLACES], on[0:8], S.rp, theirs, T.rl[:, far:far + 2]), (relays[PLACES], off, S.rp, ours, T.rl[:, near:near + 2])])

    mq = QUARTERS[r // 2]

    def spread(a, b, lists):
        return [v(V.tensor_copy(T.oo[q, 2 * a:2 * b], lists)) for q in QUARTERS][-1]

    def side(a, b, t):
        at = 128 * ORDER.index(a)
        return T.tt[:, at + t:at + 128 * (b - a):4], T.xs[:, XW * t:XW * t + XW].indirect(T.oo[:, 2 * a:2 * b])

    def gather(a, b, k=2):
        return ([v(V.tensor_copy(*side(a, b, t))) for t in range(k)][-1],
                [s(A.activation(*side(a, b, t), COPY)) for t in range(k, 4)][-1])

    def both(ready):
        V.wait_ge(S.v, ready)
        A.wait_ge(S.v, ready)

    def pack(codes, scales, at, made):
        V.wait_ge(S.v, made[0])
        V.wait_ge(S.s, made[1])
        return v(V.quantize_mx(codes[:, 0:128], scales[:, 0:128], T.tt[:, 128 * at:128 * at + 512]))
    v(V.memset(T.tt[:, 128 * ORDER.index(None):128 * ORDER.index(None) + 128], 0.0))
    V.wait_ge(S.v, v_msg)
    v_o = spread(7, 8, T.lt[mq, 47:49])
    V.wait_ge(S.s, s_xs)
    A.wait_ge(S.s, s_xs)
    both(v_o)
    gather(7, 8)
    V.wait_ge(S.lb, 8)
    both(spread(5, 7, T.li[mq, 10:14]))
    made = gather(5, 7)
    V.wait_ge(S.la, 16)
    first = spread(0, 2, T.li[mq, 0:4])
    packed = [pack(T.cb, T.db, 2, made)]
    V.wait_ge(S.lc, 24)
    second = spread(2, 5, T.li[mq, 4:10])
    both(first)
    made = [gather(0, 2)]
    both(second)
    made.append(gather(2, 5))
    packed += [pack(T.qa, T.pa, 0, made[0]), pack(T.qb, T.pb, 5, made[1])]

    for i, (h, part, runs) in enumerate(JOBS):
        if part == 0:
            g.wait_ge(S.v, packed[i // 2])
        a = 32 * (i // 4)
        src = ((T.cb, T.qa, T.qb), (T.db, T.pa, T.pb))[part][i // 2][:, a:a + 64]
        view = (u8, lambda a: a)[part]
        send([(relays[h], on, S["j%d" % i], view(src), view(stop(T, i)))])
    send([(cores[slots[4]], off, S.aa, u8(T.qb[:, 96:128]), u8(landing(T, 4)[0]))])
    send([(cores[slots[4]], off, S.aa, T.pb[:, 96:128], landing(T, 4)[1])])
    g.wait_ge(S.loc, n["loc"])

    P.wait_ge(S.v, packed[0])
    for out, a, sem, writes in ((T.m0, 64, S.ac, 2), (T.m1, 160, S.aa, 4), (T.m2, 224, S.ab, 2)):
        P.wait_ge(sem, 8 * writes)
        P.matmul_mx(out[:, 0:128], T.qw[:, :], T.pw[:, :], T.cb[:, a:a + 128], T.db[:, a:a + 128], True, True).then_inc(S.te, 1)
    A.wait_ge(S.te, 1)
    s(A.activation(T.ys[:, 0:96], T.m0[:, 32:128], COPY))
    A.wait_ge(S.te, 2)
    s_y = s(A.activation(T.ys[:, 96:192], T.m1[:, 32:128], COPY))
    V.wait_ge(S.oy, 8)
    A.wait_ge(S.oy, 8)
    V.wait_ge(S.te, 3)
    v_y = v(V.tensor_copy(T.ys[:, 192:256], T.m2[:, 64:128]))
    vw()
    V.wait_ge(S.s, s_y)
    D.wait_ge(S.v, v(V.tensor_copy(T.yo[:, 0:128], T.ys[:, :].indirect(T.oy[:, 0:8]))))
    A.wait_ge(S.v, v_y)
    A.wait_ge(S.s, s_y)
    D.wait_ge(S.s, s(A.activation(T.yo[:, 128:256], T.ys[:, :].indirect(T.oy[:, 8:16]), COPY)))
    D.dma_start(T.y[:, :], T.yo[:, :]).then_inc(S.st, 16)
    D.wait_ge(S.st, 16)
